import numpy as np
import ml_dtypes


def mxq(x, axis, fmt="e4m3"):
    dtype, down = {"e4m3": (ml_dtypes.float8_e4m3fn, 7), "e5m2": (ml_dtypes.float8_e5m2, 14)}[fmt]
    v = np.moveaxis(np.asarray(x, np.float32).astype(ml_dtypes.bfloat16).astype(np.float64), axis, -1)
    blocks = v.reshape(v.shape[:-1] + (-1, 32))
    amax = np.abs(blocks).max(-1, keepdims=True)
    byte = np.maximum(np.where(amax > 0, np.frexp(amax)[1] - 1 + 127, 0) - down, 1)
    scale = np.exp2(byte - 127.0)
    codes = (blocks / scale).astype(np.float32).astype(dtype).astype(np.float64)
    return np.moveaxis((codes * scale).reshape(v.shape), -1, axis)


WIDE = False


def mx_kscale(k):
    if not WIDE:
        return np.ones(k)
    levels = np.array([24, -24, 12, -12, 0])
    if k % 512:
        return np.exp2(np.random.permutation(np.resize(levels, k // 32))).repeat(32)
    a = np.empty((k // 512, 16))
    for p in range(k // 512):
        a[p, :8] = np.random.permutation(np.resize(levels, 8))
        for g in range(8):
            far = levels[np.abs(levels - a[p, g]) >= 10]
            a[p, g + 8] = far[np.random.randint(len(far))]
    return np.exp2(a.ravel()).repeat(32)


def f64(x):
    return np.asarray(x).astype(np.float64)


def striped8(idx):
    return np.concatenate([v.reshape(-1, 16).T for v in idx]).astype(np.uint16)


def unstriped8(offs):
    return np.stack([offs[16 * g:16 * g + 16].T.reshape(-1) for g in range(8)]).astype(np.int64)


E2M1 = np.array([0.0, 0.5, 1.0, 1.5, 2.0, 3.0, 4.0, 6.0, -0.0, -0.5, -1.0, -1.5, -2.0, -3.0, -4.0, -6.0])


def pack_weight(w, fmt):
    k, n = w.shape
    w = f64(np.asarray(w, np.float32).astype(ml_dtypes.bfloat16)).reshape(k // 32, 32, n)
    amax = np.abs(w).max(1)
    if fmt == "e4m3":
        byte = np.frexp(amax)[1] - 1 + 127 - 7
    else:
        mant, ex = np.frexp(amax / 6.0)
        byte = np.where(mant > 0.5, ex, ex - 1) + 127
    byte = np.clip(np.where(amax > 0, byte, 1), 1, 254)
    scaled = (w * np.exp2(127.0 - byte)[:, None, :]).reshape(k, n).astype(np.float32)
    by_word = np.ascontiguousarray(scaled.reshape(k // 512, 128, 4, n).transpose(0, 1, 3, 2))
    if fmt == "e4m3":
        words = by_word.astype(ml_dtypes.float8_e4m3fn).view(np.uint8)
    else:
        c = by_word.astype(ml_dtypes.float4_e2m1fn).view(np.uint8) & 0xF
        words = (c[..., 0::2] | (c[..., 1::2] << 4)).reshape(k // 512, 128, 2 * n)
    return np.ascontiguousarray(words), np.ascontiguousarray(byte.astype(np.uint8).reshape(k // 512, 16, n))


def unpack_weight(words, scales, fmt):
    g, _, n = scales.shape
    words = np.ascontiguousarray(words).reshape(g, 128, n, -1)
    if fmt == "e4m3":
        vals = words.view(ml_dtypes.float8_e4m3fn).astype(np.float64)
    else:
        nib = np.empty((g, 128, n, 4), np.uint8)
        nib[..., 0::2] = words & 0xF
        nib[..., 1::2] = words >> 4
        vals = E2M1[nib]
    vals = vals * np.repeat(np.exp2(scales.astype(np.float64) - 127.0), 8, axis=1)[..., None]
    return vals.transpose(0, 1, 3, 2).reshape(g * 512, n)


def planes(y):
    n, m = y.shape
    v = y.astype(np.float32).astype(ml_dtypes.bfloat16).astype(np.float64).reshape(n // 32, 32, m)
    top = np.abs(v).max(1)
    byte = np.clip(np.where(top > 0, np.frexp(top)[1] - 1 + 127 - 7, 1), 1, 254)
    codes = (v * np.exp2(127.0 - byte)[:, None, :]).reshape(n, m).astype(np.float32).astype(ml_dtypes.float8_e4m3fn).view(np.uint8)
    words = codes.reshape(n // 512, 128, 4, m).transpose(0, 1, 3, 2)
    return np.ascontiguousarray(words), np.ascontiguousarray(byte.astype(np.uint8).reshape(n // 512, 16, m))


def gelu(f):
    return 0.5 * f * (1.0 + np.tanh(np.sqrt(2.0 / np.pi) * (f + 0.044715 * f**3)))


K, R, N, T, J = 1024, 1024, 512, 2048, 1024


def setup_inputs():
    n = np.random.standard_normal
    s = mx_kscale(K)[:, None]
    u = mx_kscale(R)[:, None]
    wd = n((R, N)) / np.sqrt(R) / u
    p_wu = pack_weight(n((K, R)) / np.sqrt(K) / s * u.T, "e2m1")
    p_wd8 = pack_weight(wd[:512], "e4m3")
    p_wd4 = pack_weight(wd[512:], "e2m1")
    return {
        "xT": (n((K, T)) * s).astype(np.float32),
        "wgt": np.repeat(np.random.uniform(0.5, 2.0, (8, J)), 16, axis=0).astype(np.float32),
        "wg": (n((K, R)) / np.sqrt(K) / s).astype(np.float32),
        "wu_words": p_wu[0],
        "wu_scales": p_wu[1],
        "wd8_words": p_wd8[0],
        "wd8_scales": p_wd8[1],
        "wd4_words": p_wd4[0],
        "wd4_scales": p_wd4[1],
        "b": (0.3 * n(N)).astype(np.float32),
        "offs": striped8(np.stack([np.random.permutation(T)[:J] for _ in range(8)])),
    }


def reference(xT, wgt, wg, wu_words, wu_scales, wd8_words, wd8_scales, wd4_words, wd4_scales, b, offs):
    idx = unstriped8(offs)
    rows = np.arange(K)
    xg = f64(wgt)[rows // 4 % 128] * f64(xT)[rows[:, None], idx[rows % 512 // 64]]
    xT_ = mxq(xg, 0, "e4m3")
    wg_ = mxq(f64(wg), 0, "e4m3")
    wu_ = unpack_weight(wu_words, wu_scales, "e2m1")
    ga = wg_.T @ xT_
    ub = wu_.T @ xT_
    h = gelu(ga) * ub
    h_ = mxq(h, 0, "e4m3")
    wd8_ = unpack_weight(wd8_words, wd8_scales, "e4m3")
    wd4_ = unpack_weight(wd4_words, wd4_scales, "e2m1")
    y = wd8_.T @ h_[:512] + wd4_.T @ h_[512:]
    out_0 = y + f64(b)[:, None]
    return (out_0,) + planes(out_0)

@@ -1,0 +1,301 @@
+from contextlib import ExitStack
+
+import concourse.mybir as mybir
+
+K, R, N, T, J = 1024, 1024, 512, 2048, 1024
+FLOPS = 2 * J * (2 * K * R + R * N)
+
+F32 = mybir.dt.float32
+BF16 = mybir.dt.bfloat16
+I32 = mybir.dt.int32
+U16 = mybir.dt.uint16
+U8 = mybir.dt.uint8
+FP8X4 = mybir.dt.float8_e4m3fn_x4
+FP4X4 = mybir.dt.float4_e2m1fn_x4
+MULT = mybir.AluOpType.mult
+GELU = mybir.ActivationFunctionType.Gelu_apprx_tanh
+IDENTITY = mybir.ActivationFunctionType.Identity
+
+P = 128
+PASS = 512
+UNIT = 256
+OUT_CHUNKS = ((0, 512), (512, 256), (768, 128), (896, 128))
+
+
+def interleave(copy, words, planes):
+    copy(out=words.rearrange("p (c i t) -> p c t i", i=4, t=4), in_=planes.rearrange("p t (c i) -> p c t i", i=4))
+
+
+def tile_list_gelu_mix_biasP_kernel(
+    tc, xT, wgt, wg, wu_words, wu_scales, wd8_words, wd8_scales, wd4_words, wd4_scales, b, offs, out_0, out_1, out_2
+):
+    nc = tc.nc
+    with ExitStack() as ctx:
+        keep = ctx.enter_context(tc.tile_pool(name="keep", bufs=1))
+        ring2 = ctx.enter_context(tc.tile_pool(name="ring2", bufs=2))
+        ring3 = ctx.enter_context(tc.tile_pool(name="ring3", bufs=3))
+        psum = ctx.enter_context(tc.psum_pool(name="psum", bufs=4))
+
+        def kept(name, shape, dtype):
+            return keep.tile(shape, dtype, name=name, align_bytes=64)
+
+        offsets = keep.tile([P, J // 16], U16, name="offsets")
+        nc.sync.dma_start(offsets[:], offs)
+
+        wu_scale_raw = kept("wu_scale_raw", [P, 2, R], U8)
+        wd_scale_raw = kept("wd_scale_raw", [P, 2, N], U8)
+        nc.vector.memset(wu_scale_raw[:].bitcast(I32), 0)
+        for q in range(4):
+            nc.scalar.dma_start(
+                out=wu_scale_raw[32 * q : 32 * q + 4, :, :].bitcast(I32),
+                in_=wu_scales[:, 4 * q : 4 * q + 4, :].rearrange("a q r -> q a r").bitcast(I32),
+            )
+        nc.vector.memset(wd_scale_raw[:].bitcast(I32), 0)
+
+        place_w = [kept("place_w%d" % h, [P, 512], F32) for h in range(2)]
+        x_planes = [[kept("x_plane%d%d" % (a, i), [P, T], F32) for i in range(4)] for a in range(2)]
+        wu_raw = [kept("wu_raw%d" % g, [P, 2, 2 * PASS], U8) for g in range(2)]
+        wg_raw = {}
+
+        def load_plane(a, i):
+            rows = xT[a * PASS : (a + 1) * PASS, :].rearrange("(p i) t -> p i t", i=4)
+            nc.sync.dma_start(out=x_planes[a][i][:], in_=rows[:, i, :])
+
+        def load_wg(a, g):
+            raw = ring3.tile([P, 4, PASS], F32, name="f32_stage")
+            rows = wg[a * PASS : (a + 1) * PASS, g * PASS : (g + 1) * PASS]
+            nc.sync.dma_start(out=raw[:], in_=rows.rearrange("(p i) r -> p i r", i=4))
+            wg_raw[(a, g)] = raw
+
+        def load_wu(g):
+            cols = wu_words[:, :, 2 * g * PASS : 2 * (g + 1) * PASS]
+            nc.sync.dma_start(out=wu_raw[g][:].bitcast(I32), in_=cols.rearrange("a p c -> p a c").bitcast(I32))
+
+        nc.sync.dma_start(out=place_w[0][:], in_=wgt[:, 0:512])
+        load_plane(0, 0)
+        nc.sync.dma_start(out=place_w[1][:], in_=wgt[:, 512:1024])
+        load_wu(0)
+        load_plane(0, 1)
+        load_plane(0, 2)
+        load_plane(0, 3)
+        load_wg(0, 0)
+        for i in range(4):
+            load_plane(1, i)
+        load_wg(1, 0)
+        load_wu(1)
+        load_wg(0, 1)
+        load_wg(1, 1)
+
+        wd8_raw = kept("wd8_raw", [P, N], I32)
+        wd4_raw = kept("wd4_raw", [P, 2 * N], U8)
+        bias = kept("bias", [P, 4], F32)
+        nc.sync.dma_start(out=wd8_raw[:], in_=wd8_words[0].rearrange("p n i -> p (n i)").bitcast(I32))
+        nc.sync.dma_start(out=wd4_raw[:].bitcast(I32), in_=wd4_words[0].bitcast(I32))
+        nc.sync.dma_start(out=bias[:], in_=b.rearrange("(p t) -> p t", t=4))
+        for half, scales in enumerate((wd8_scales, wd4_scales)):
+            for q in range(4):
+                nc.sync.dma_start(
+                    out=wd_scale_raw[32 * q : 32 * q + 4, half, :].bitcast(I32),
+                    in_=scales[0, 4 * q : 4 * q + 4, :].bitcast(I32),
+                )
+
+        x_codes = [kept("x_codes%d" % a, [P, J], I32) for a in range(2)]
+        x_scales = [kept("x_scales%d" % a, [P, J], U8) for a in range(2)]
+        wg_codes, wg_scales = {}, {}
+        wu_dealt = [kept("wu_dealt%d" % g, [P, 2 * 2 * PASS], U8) for g in range(2)]
+        wu_scale = [kept("wu_scale%d" % g, [P, 2 * PASS], U8) for g in range(2)]
+        wd8_dealt = kept("wd8_dealt", [P, N], I32)
+        wd4_dealt = kept("wd4_dealt", [P, 2 * N], U8)
+        wd_scale = kept("wd_scale", [P, 2 * N], U8)
+
+        def gather(picked, a, i, j0, width):
+            h, c0 = divmod(j0, 512)
+            nc.vector.tensor_tensor(
+                picked[:, i, :],
+                x_planes[a][i][:].indirect(offsets[:, j0 // 16 : (j0 + width) // 16]),
+                place_w[h][:, c0 : c0 + width],
+                MULT,
+            )
+
+        def quantise_x(picked, a, j0, width):
+            words = ring3.tile([P, 4 * width], BF16, name="x_words", align_bytes=64)
+            interleave(nc.scalar.copy, words[:], picked[:])
+            nc.vector.quantize_mx(
+                out=x_codes[a][:, j0 : j0 + width].bitcast(FP8X4), scales=x_scales[a][:, j0 : j0 + width], in_=words[:]
+            )
+
+        def quantise_wg(a, g, vector_share):
+            words = ring2.tile([P, 4 * PASS], BF16, name="wg_words", align_bytes=64)
+            dealt = words[:].rearrange("p (t m i) -> p m i t", t=4, i=4)
+            raw = wg_raw[(a, g)][:].rearrange("p i (m t) -> p m i t", t=4)
+            split = P - vector_share
+            nc.scalar.copy(out=dealt[:, 0:split], in_=raw[:, 0:split])
+            if vector_share:
+                nc.vector.tensor_copy(out=dealt[:, split:P], in_=raw[:, split:P])
+            wg_codes[(a, g)] = kept("wg_codes%d%d" % (a, g), [P, PASS], I32)
+            wg_scales[(a, g)] = kept("wg_scales%d%d" % (a, g), [P, PASS], U8)
+            nc.vector.quantize_mx(out=wg_codes[(a, g)][:].bitcast(FP8X4), scales=wg_scales[(a, g)][:], in_=words[:])
+
+        def deal_wu(g):
+            nc.vector.tensor_copy(
+                out=wu_dealt[g][:].rearrange("p (a t m e) -> p a t m e", a=2, t=4, e=2),
+                in_=wu_raw[g][:].rearrange("p a (m t e) -> p a t m e", t=4, e=2),
+            )
+            nc.vector.tensor_copy(
+                out=wu_scale[g][:].rearrange("p (a t m) -> p a t m", a=2, t=4),
+                in_=wu_scale_raw[:, :, g * PASS : (g + 1) * PASS].rearrange("p a (m t) -> p a t m", t=4),
+            )
+
+        def deal_wd():
+            nc.vector.tensor_copy(
+                out=wd8_dealt[:].rearrange("p (t m) -> p t m", t=4), in_=wd8_raw[:].rearrange("p (m t) -> p t m", t=4)
+            )
+            nc.vector.tensor_copy(
+                out=wd4_dealt[:].rearrange("p (t m e) -> p t m e", t=4, e=2),
+                in_=wd4_raw[:].rearrange("p (m t e) -> p t m e", t=4, e=2),
+            )
+            nc.vector.tensor_copy(
+                out=wd_scale[:].rearrange("p (a t m) -> p a t m", a=2, t=4),
+                in_=wd_scale_raw[:].rearrange("p a (m t) -> p a t m", t=4),
+            )
+
+        picked0 = [kept("picked0%d" % h, [P, 4, 512], F32) for h in range(2)]
+        picked1 = [kept("picked1%d" % u, [P, 4, UNIT], F32) for u in range(J // UNIT)]
+        for i in range(4):
+            for h in range(2):
+                gather(picked0[h], 0, i, 512 * h, 512)
+            if i == 0:
+                deal_wu(0)
+        for h in range(2):
+            quantise_x(picked0[h], 0, 512 * h, 512)
+        quantise_wg(0, 0, 0)
+        for i in range(3):
+            for u in range(J // UNIT):
+                gather(picked1[u], 1, i, UNIT * u, UNIT)
+        for u in range(J // UNIT):
+            gather(picked1[u], 1, 3, UNIT * u, UNIT)
+            quantise_x(picked1[u], 1, UNIT * u, UNIT)
+        quantise_wg(1, 0, 64)
+
+        h_codes = [kept("h_codes%d" % g, [P, J], I32) for g in range(2)]
+        h_scales = [kept("h_scales%d" % g, [P, J], U8) for g in range(2)]
+        y_codes = kept("y_codes", [P, J], I32)
+        y_scales = kept("y_scales", [P, J], U8)
+
+        def hidden_unit(g, u):
+            j0 = UNIT * u
+            gated = ring3.tile([P, 2, UNIT, 2], F32, name="gated")
+            for pair in range(2):
+                bank = psum.tile([P, 2, UNIT], F32, name="gate_bank")
+                for a in range(2):
+                    for e in range(2):
+                        cols = slice(P * (2 * pair + e), P * (2 * pair + e + 1))
+                        nc.tensor.matmul_mx(
+                            out=bank[:, e, :],
+                            lhsT=wg_codes[(a, g)][:, cols].bitcast(FP8X4),
+                            lhsT_scale=wg_scales[(a, g)][:, cols],
+                            rhs=x_codes[a][:, j0 : j0 + UNIT].bitcast(FP8X4),
+                            rhs_scale=x_scales[a][:, j0 : j0 + UNIT],
+                            start=(a == 0 and e == 0),
+                            stop=(a == 1 and e == 1),
+                        )
+                nc.scalar.activation(out=gated[:, pair, :, :], in_=bank[:].rearrange("p e j -> p j e"), func=GELU)
+            h_words = ring3.tile([P, 4 * UNIT], BF16, name="h_words", align_bytes=64)
+            for c in range(UNIT // P):
+                bank = psum.tile([P, 4, P], F32, name="up_bank")
+                places = slice(j0 + P * c, j0 + P * (c + 1))
+                for a in range(2):
+                    for t in range(4):
+                        s = 4 * a + t
+                        nc.tensor.matmul_mx(
+                            out=bank[:, t, :],
+                            lhsT=wu_dealt[g][:, 2 * P * s : 2 * P * (s + 1)].bitcast(FP4X4),
+                            lhsT_scale=wu_scale[g][:, P * s : P * (s + 1)],
+                            rhs=x_codes[a][:, places].bitcast(FP8X4),
+                            rhs_scale=x_scales[a][:, places],
+                            start=(s == 0),
+                            stop=(s == 7),
+                        )
+                nc.vector.tensor_tensor(
+                    h_words[:, 4 * P * c : 4 * P * (c + 1)].rearrange("p (j q e) -> p j q e", q=2, e=2),
+                    bank[:].rearrange("p (q e) j -> p j q e", q=2),
+                    gated[:, :, P * c : P * (c + 1), :].rearrange("p q j e -> p j q e"),
+                    MULT,
+                )
+            last = g == 1 and u == J // UNIT - 1
+            step = P if last else UNIT
+            for c0 in range(0, UNIT, step):
+                places = slice(j0 + c0, j0 + c0 + step)
+                nc.vector.quantize_mx(
+                    out=h_codes[g][:, places].bitcast(FP8X4),
+                    scales=h_scales[g][:, places],
+                    in_=h_words[:, 4 * c0 : 4 * (c0 + step)],
+                )
+
+        y_rows = out_0.rearrange("(p t) j -> p t j", t=4)
+        y_word_rows = out_1[0].rearrange("p j i -> p (j i)").bitcast(I32)
+
+        def output_chunk(j0, width):
+            places = slice(j0, j0 + width)
+            y = ring3.tile([P, 4, width], F32, name="f32_stage")
+            per_bank = 512 // width
+            for t0 in range(0, 4, per_bank):
+                bank = psum.tile([P, per_bank, width], F32, name="gate_bank" if (t0 // per_bank) % 2 == 0 else "up_bank")
+                for t in range(t0, t0 + per_bank):
+                    nc.tensor.matmul_mx(
+                        out=bank[:, t - t0, :],
+                        lhsT=wd8_dealt[:, P * t : P * (t + 1)].bitcast(FP8X4),
+                        lhsT_scale=wd_scale[:, P * t : P * (t + 1)],
+                        rhs=h_codes[0][:, places].bitcast(FP8X4),
+                        rhs_scale=h_scales[0][:, places],
+                        start=(t == t0),
+                        stop=False,
+                    )
+                step = 512 if width == 512 else P
+                for t in range(t0, t0 + per_bank):
+                    for c0 in range(0, width, step):
+                        part = slice(j0 + c0, j0 + c0 + step)
+                        nc.tensor.matmul_mx(
+                            out=bank[:, t - t0, c0 : c0 + step],
+                            lhsT=wd4_dealt[:, 2 * P * t : 2 * P * (t + 1)].bitcast(FP4X4),
+                            lhsT_scale=wd_scale[:, N + P * t : N + P * (t + 1)],
+                            rhs=h_codes[1][:, part].bitcast(FP8X4),
+                            rhs_scale=h_scales[1][:, part],
+                            start=False,
+                            stop=(t == t0 + per_bank - 1 and c0 + step == width),
+                        )
+                for t in range(t0, t0 + per_bank):
+                    nc.scalar.activation(
+                        out=y[:, t, :], in_=bank[:, t - t0, :], func=IDENTITY, bias=bias[:, t : t + 1], scale=1.0
+                    )
+            nc.sync.dma_start(out=y_rows[:, :, places], in_=y[:])
+            y_words = ring2.tile([P, 4 * width], BF16, name="y_words", align_bytes=64)
+            interleave(nc.vector.tensor_copy, y_words[:], y[:])
+            nc.vector.quantize_mx(out=y_codes[:, places].bitcast(FP8X4), scales=y_scales[:, places], in_=y_words[:])
+            nc.sync.dma_start(out=y_word_rows[:, places], in_=y_codes[:, places])
+
+        def store_scales(j0, width):
+            for q in range(4):
+                nc.sync.dma_start(
+                    out=out_2[0, 4 * q : 4 * q + 4, j0 : j0 + width].bitcast(I32),
+                    in_=y_scales[32 * q : 32 * q + 4, j0 : j0 + width].bitcast(I32),
+                )
+
+        hidden_unit(0, 0)
+        hidden_unit(0, 1)
+        deal_wu(1)
+        quantise_wg(0, 1, 0)
+        hidden_unit(0, 2)
+        quantise_wg(1, 1, 0)
+        hidden_unit(0, 3)
+        deal_wd()
+        hidden_unit(1, 0)
+        hidden_unit(1, 1)
+        hidden_unit(1, 2)
+        output_chunk(*OUT_CHUNKS[0])
+        hidden_unit(1, 3)
+        output_chunk(*OUT_CHUNKS[1])
+        store_scales(0, 768)
+        output_chunk(*OUT_CHUNKS[2])
+        output_chunk(*OUT_CHUNKS[3])
+        store_scales(768, 256)

@@ -13,17 +13,23 @@ U8 = mybir.dt.uint8
 FP8X4 = mybir.dt.float8_e4m3fn_x4
 FP4X4 = mybir.dt.float4_e2m1fn_x4
 MULT = mybir.AluOpType.mult
+ADD = mybir.AluOpType.add
 GELU = mybir.ActivationFunctionType.Gelu_apprx_tanh
 IDENTITY = mybir.ActivationFunctionType.Identity
 
 P = 128
 PASS = 512
+BANK = 512
+HALF = J // 2
 UNIT = 256
-OUT_CHUNKS = ((0, 512), (512, 256), (768, 128), (896, 128))
 
 
-def interleave(copy, words, planes):
-    copy(out=words.rearrange("p (c i t) -> p c t i", i=4, t=4), in_=planes.rearrange("p t (c i) -> p c t i", i=4))
+def as_words(words):
+    return words.rearrange("p (c e t) -> p c t e", e=2, t=4)
+
+
+def as_planes(planes):
+    return planes.rearrange("p t (c e) -> p c t e", e=2)
 
 
 def tile_list_gelu_mix_biasP_kernel(
@@ -45,16 +51,14 @@ def tile_list_gelu_mix_biasP_kernel(
         wu_scale_raw = kept("wu_scale_raw", [P, 2, R], U8)
         wd_scale_raw = kept("wd_scale_raw", [P, 2, N], U8)
         nc.vector.memset(wu_scale_raw[:].bitcast(I32), 0)
-        for q in range(4):
-            nc.scalar.dma_start(
-                out=wu_scale_raw[32 * q : 32 * q + 4, :, :].bitcast(I32),
-                in_=wu_scales[:, 4 * q : 4 * q + 4, :].rearrange("a q r -> q a r").bitcast(I32),
-            )
         nc.vector.memset(wd_scale_raw[:].bitcast(I32), 0)
 
-        place_w = [kept("place_w%d" % h, [P, 512], F32) for h in range(2)]
+        place_w = [kept("place_w%d" % half, [P, HALF], F32) for half in range(2)]
         x_planes = [[kept("x_plane%d%d" % (a, i), [P, T], F32) for i in range(4)] for a in range(2)]
         wu_raw = [kept("wu_raw%d" % g, [P, 2, 2 * PASS], U8) for g in range(2)]
+        wd8_raw = kept("wd8_raw", [P, N], I32)
+        wd4_raw = kept("wd4_raw", [P, 2 * N], U8)
+        bias = kept("bias", [P, 4], F32)
         wg_raw = {}
 
         def load_plane(a, i):
@@ -71,31 +75,32 @@ def tile_list_gelu_mix_biasP_kernel(
             cols = wu_words[:, :, 2 * g * PASS : 2 * (g + 1) * PASS]
             nc.sync.dma_start(out=wu_raw[g][:].bitcast(I32), in_=cols.rearrange("a p c -> p a c").bitcast(I32))
 
-        nc.sync.dma_start(out=place_w[0][:], in_=wgt[:, 0:512])
-        load_plane(0, 0)
-        nc.sync.dma_start(out=place_w[1][:], in_=wgt[:, 512:1024])
         load_wu(0)
-        load_plane(0, 1)
-        load_plane(0, 2)
-        load_plane(0, 3)
-        load_wg(0, 0)
-        for i in range(4):
-            load_plane(1, i)
-        load_wg(1, 0)
+        for q in range(4):
+            nc.sync.dma_start(
+                out=wu_scale_raw[32 * q : 32 * q + 4, :, :].bitcast(I32),
+                in_=wu_scales[:, 4 * q : 4 * q + 4, :].rearrange("a q r -> q a r").bitcast(I32),
+            )
+        nc.sync.dma_start(out=place_w[0][:], in_=wgt[:, 0:HALF])
+        load_plane(0, 0)
+        nc.sync.dma_start(out=place_w[1][:], in_=wgt[:, HALF:J])
         load_wu(1)
-        load_wg(0, 1)
+        for i in range(1, 4):
+            load_plane(0, i)
+        for i in range(3):
+            load_plane(1, i)
+        load_wg(0, 0)
+        load_plane(1, 3)
+        load_wg(1, 0)
         load_wg(1, 1)
-
-        wd8_raw = kept("wd8_raw", [P, N], I32)
-        wd4_raw = kept("wd4_raw", [P, 2 * N], U8)
-        bias = kept("bias", [P, 4], F32)
+        load_wg(0, 1)
         nc.sync.dma_start(out=wd8_raw[:], in_=wd8_words[0].rearrange("p n i -> p (n i)").bitcast(I32))
         nc.sync.dma_start(out=wd4_raw[:].bitcast(I32), in_=wd4_words[0].bitcast(I32))
         nc.sync.dma_start(out=bias[:], in_=b.rearrange("(p t) -> p t", t=4))
-        for half, scales in enumerate((wd8_scales, wd4_scales)):
+        for g, scales in enumerate((wd8_scales, wd4_scales)):
             for q in range(4):
                 nc.sync.dma_start(
-                    out=wd_scale_raw[32 * q : 32 * q + 4, half, :].bitcast(I32),
+                    out=wd_scale_raw[32 * q : 32 * q + 4, g, :].bitcast(I32),
                     in_=scales[0, 4 * q : 4 * q + 4, :].bitcast(I32),
                 )
 
@@ -107,39 +112,39 @@ def tile_list_gelu_mix_biasP_kernel(
         wd8_dealt = kept("wd8_dealt", [P, N], I32)
         wd4_dealt = kept("wd4_dealt", [P, 2 * N], U8)
         wd_scale = kept("wd_scale", [P, 2 * N], U8)
+        picked = [[kept("picked%d%d" % (a, half), [P, 4, HALF], F32) for half in range(2)] for a in range(2)]
 
-        def gather(picked, a, i, j0, width):
-            h, c0 = divmod(j0, 512)
+        def gather(a, i, j0, width):
+            half, c0 = divmod(j0, HALF)
             nc.vector.tensor_tensor(
-                picked[:, i, :],
+                picked[a][half][:, i, c0 : c0 + width],
                 x_planes[a][i][:].indirect(offsets[:, j0 // 16 : (j0 + width) // 16]),
-                place_w[h][:, c0 : c0 + width],
+                place_w[half][:, c0 : c0 + width],
                 MULT,
             )
 
-        def quantise_x(picked, a, j0, width):
+        def quantise_x(a, j0, width):
+            half, c0 = divmod(j0, HALF)
             words = ring3.tile([P, 4 * width], BF16, name="x_words", align_bytes=64)
-            interleave(nc.scalar.copy, words[:], picked[:])
-            nc.vector.quantize_mx(
-                out=x_codes[a][:, j0 : j0 + width].bitcast(FP8X4), scales=x_scales[a][:, j0 : j0 + width], in_=words[:]
-            )
+            nc.scalar.copy(out=as_words(words[:]), in_=as_planes(picked[a][half][:, :, c0 : c0 + width]))
+            places = slice(j0, j0 + width)
+            nc.vector.quantize_mx(out=x_codes[a][:, places].bitcast(FP8X4), scales=x_scales[a][:, places], in_=words[:])
 
-        def quantise_wg(a, g, vector_share):
+        def quantise_wg(a, g, copy, pieces):
             words = ring2.tile([P, 4 * PASS], BF16, name="wg_words", align_bytes=64)
-            dealt = words[:].rearrange("p (t m i) -> p m i t", t=4, i=4)
-            raw = wg_raw[(a, g)][:].rearrange("p i (m t) -> p m i t", t=4)
-            split = P - vector_share
-            nc.scalar.copy(out=dealt[:, 0:split], in_=raw[:, 0:split])
-            if vector_share:
-                nc.vector.tensor_copy(out=dealt[:, split:P], in_=raw[:, split:P])
+            dealt = words[:].rearrange("p (u e m i) -> p u m i e", u=2, e=2, i=4)
+            raw = wg_raw[(a, g)][:].rearrange("p i (m u e) -> p u m i e", u=2, e=2)
+            step = P // pieces
+            for m0 in range(0, P, step):
+                copy(out=dealt[:, :, m0 : m0 + step], in_=raw[:, :, m0 : m0 + step])
             wg_codes[(a, g)] = kept("wg_codes%d%d" % (a, g), [P, PASS], I32)
             wg_scales[(a, g)] = kept("wg_scales%d%d" % (a, g), [P, PASS], U8)
             nc.vector.quantize_mx(out=wg_codes[(a, g)][:].bitcast(FP8X4), scales=wg_scales[(a, g)][:], in_=words[:])
 
         def deal_wu(g):
             nc.vector.tensor_copy(
-                out=wu_dealt[g][:].rearrange("p (a t m e) -> p a t m e", a=2, t=4, e=2),
-                in_=wu_raw[g][:].rearrange("p a (m t e) -> p a t m e", t=4, e=2),
+                out=wu_dealt[g][:].bitcast(U16).rearrange("p (a t m) -> p a t m", a=2, t=4),
+                in_=wu_raw[g][:].bitcast(U16).rearrange("p a (m t) -> p a t m", t=4),
             )
             nc.vector.tensor_copy(
                 out=wu_scale[g][:].rearrange("p (a t m) -> p a t m", a=2, t=4),
@@ -148,154 +153,152 @@ def tile_list_gelu_mix_biasP_kernel(
 
         def deal_wd():
             nc.vector.tensor_copy(
-                out=wd8_dealt[:].rearrange("p (t m) -> p t m", t=4), in_=wd8_raw[:].rearrange("p (m t) -> p t m", t=4)
+                out=wd8_dealt[:].rearrange("p (u e m) -> p u m e", u=2, e=2),
+                in_=wd8_raw[:].rearrange("p (m u e) -> p u m e", u=2, e=2),
             )
             nc.vector.tensor_copy(
-                out=wd4_dealt[:].rearrange("p (t m e) -> p t m e", t=4, e=2),
-                in_=wd4_raw[:].rearrange("p (m t e) -> p t m e", t=4, e=2),
+                out=wd4_dealt[:].bitcast(U16).rearrange("p (t m) -> p t m", t=4),
+                in_=wd4_raw[:].bitcast(U16).rearrange("p (m t) -> p t m", t=4),
             )
             nc.vector.tensor_copy(
-                out=wd_scale[:].rearrange("p (a t m) -> p a t m", a=2, t=4),
-                in_=wd_scale_raw[:].rearrange("p a (m t) -> p a t m", t=4),
+                out=wd_scale[:].rearrange("p (g t m) -> p g t m", g=2, t=4),
+                in_=wd_scale_raw[:].rearrange("p g (m t) -> p g t m", t=4),
             )
 
-        picked0 = [kept("picked0%d" % h, [P, 4, 512], F32) for h in range(2)]
-        picked1 = [kept("picked1%d" % u, [P, 4, UNIT], F32) for u in range(J // UNIT)]
+        deal_wu(0)
+        deal_wu(1)
         for i in range(4):
-            for h in range(2):
-                gather(picked0[h], 0, i, 512 * h, 512)
-            if i == 0:
-                deal_wu(0)
-        for h in range(2):
-            quantise_x(picked0[h], 0, 512 * h, 512)
-        quantise_wg(0, 0, 0)
+            for j0 in range(0, J, HALF):
+                gather(0, i, j0, HALF)
+        for j0 in range(0, J, HALF):
+            quantise_x(0, j0, HALF)
+        quantise_wg(0, 0, nc.scalar.copy, 1)
         for i in range(3):
-            for u in range(J // UNIT):
-                gather(picked1[u], 1, i, UNIT * u, UNIT)
-        for u in range(J // UNIT):
-            gather(picked1[u], 1, 3, UNIT * u, UNIT)
-            quantise_x(picked1[u], 1, UNIT * u, UNIT)
-        quantise_wg(1, 0, 64)
+            for j0 in range(0, J, HALF):
+                gather(1, i, j0, HALF)
+        quantise_wg(1, 0, nc.vector.tensor_copy, 2)
+        for j0 in range(0, J, UNIT):
+            gather(1, 3, j0, UNIT)
+            quantise_x(1, j0, UNIT)
 
         h_codes = [kept("h_codes%d" % g, [P, J], I32) for g in range(2)]
         h_scales = [kept("h_scales%d" % g, [P, J], U8) for g in range(2)]
         y_codes = kept("y_codes", [P, J], I32)
         y_scales = kept("y_scales", [P, J], U8)
 
-        def hidden_unit(g, u):
-            j0 = UNIT * u
-            gated = ring3.tile([P, 2, UNIT, 2], F32, name="gated")
-            for pair in range(2):
-                bank = psum.tile([P, 2, UNIT], F32, name="gate_bank")
-                for a in range(2):
-                    for e in range(2):
-                        cols = slice(P * (2 * pair + e), P * (2 * pair + e + 1))
+        def hidden_unit(g, j0, width):
+            passes = (0, 1) if g == 0 and j0 < 2 * UNIT else (1, 0)
+            places = slice(j0, j0 + width)
+            gated = ring3.tile([P, 4, width], F32, name="gated")
+            per_bank = BANK // width
+            for t0 in range(0, 4, per_bank):
+                bank = psum.tile([P, per_bank, width], F32, name="gate_bank")
+                for a in passes:
+                    for s in range(per_bank):
+                        cols = slice(P * (t0 + s), P * (t0 + s + 1))
                         nc.tensor.matmul_mx(
-                            out=bank[:, e, :],
+                            out=bank[:, s, :],
                             lhsT=wg_codes[(a, g)][:, cols].bitcast(FP8X4),
                             lhsT_scale=wg_scales[(a, g)][:, cols],
-                            rhs=x_codes[a][:, j0 : j0 + UNIT].bitcast(FP8X4),
-                            rhs_scale=x_scales[a][:, j0 : j0 + UNIT],
-                            start=(a == 0 and e == 0),
-                            stop=(a == 1 and e == 1),
-                        )
-                nc.scalar.activation(out=gated[:, pair, :, :], in_=bank[:].rearrange("p e j -> p j e"), func=GELU)
-            h_words = ring3.tile([P, 4 * UNIT], BF16, name="h_words", align_bytes=64)
-            for c in range(UNIT // P):
-                bank = psum.tile([P, 4, P], F32, name="up_bank")
-                places = slice(j0 + P * c, j0 + P * (c + 1))
-                for a in range(2):
-                    for t in range(4):
-                        s = 4 * a + t
-                        nc.tensor.matmul_mx(
-                            out=bank[:, t, :],
-                            lhsT=wu_dealt[g][:, 2 * P * s : 2 * P * (s + 1)].bitcast(FP4X4),
-                            lhsT_scale=wu_scale[g][:, P * s : P * (s + 1)],
                             rhs=x_codes[a][:, places].bitcast(FP8X4),
                             rhs_scale=x_scales[a][:, places],
-                            start=(s == 0),
-                            stop=(s == 7),
+                            start=(a == passes[0] and s == 0),
+                            stop=(a == passes[1] and s == per_bank - 1),
+                        )
+                nc.scalar.activation(out=gated[:, t0 : t0 + per_bank, :], in_=bank[:], func=GELU)
+            h_words = ring3.tile([P, 4 * width], BF16, name="h_words", align_bytes=64)
+            for c0 in range(0, width, P):
+                bank = psum.tile([P, 4, P], F32, name="up_bank")
+                part = slice(j0 + c0, j0 + c0 + P)
+                for a in passes:
+                    for t in range(4):
+                        col0 = PASS * a + P * t
+                        nc.tensor.matmul_mx(
+                            out=bank[:, t, :],
+                            lhsT=wu_dealt[g][:, 2 * col0 : 2 * (col0 + P)].bitcast(FP4X4),
+                            lhsT_scale=wu_scale[g][:, col0 : col0 + P],
+                            rhs=x_codes[a][:, part].bitcast(FP8X4),
+                            rhs_scale=x_scales[a][:, part],
+                            start=(a == passes[0] and t == 0),
+                            stop=(a == passes[1] and t == 3),
                         )
                 nc.vector.tensor_tensor(
-                    h_words[:, 4 * P * c : 4 * P * (c + 1)].rearrange("p (j q e) -> p j q e", q=2, e=2),
-                    bank[:].rearrange("p (q e) j -> p j q e", q=2),
-                    gated[:, :, P * c : P * (c + 1), :].rearrange("p q j e -> p j q e"),
+                    as_words(h_words[:, 4 * c0 : 4 * (c0 + P)]),
+                    as_planes(bank[:]),
+                    as_planes(gated[:, :, c0 : c0 + P]),
                     MULT,
                 )
-            last = g == 1 and u == J // UNIT - 1
-            step = P if last else UNIT
-            for c0 in range(0, UNIT, step):
-                places = slice(j0 + c0, j0 + c0 + step)
-                nc.vector.quantize_mx(
-                    out=h_codes[g][:, places].bitcast(FP8X4),
-                    scales=h_scales[g][:, places],
-                    in_=h_words[:, 4 * c0 : 4 * (c0 + step)],
-                )
+            nc.vector.quantize_mx(out=h_codes[g][:, places].bitcast(FP8X4), scales=h_scales[g][:, places], in_=h_words[:])
 
         y_rows = out_0.rearrange("(p t) j -> p t j", t=4)
         y_word_rows = out_1[0].rearrange("p j i -> p (j i)").bitcast(I32)
 
+        def wd8_passes(bank, t0, j0, width, first):
+            for s in range(2):
+                cols = slice(P * (t0 + s), P * (t0 + s + 1))
+                nc.tensor.matmul_mx(
+                    out=bank[:, s, :],
+                    lhsT=wd8_dealt[:, cols].bitcast(FP8X4),
+                    lhsT_scale=wd_scale[:, cols],
+                    rhs=h_codes[0][:, j0 : j0 + width].bitcast(FP8X4),
+                    rhs_scale=h_scales[0][:, j0 : j0 + width],
+                    start=(first and s == 0),
+                    stop=(not first and s == 1),
+                )
+
+        def wd4_passes(bank, t0, j0, width, first):
+            for s in range(2):
+                col0 = P * (t0 + s)
+                for c0 in range(0, width, P):
+                    part = slice(j0 + c0, j0 + c0 + P)
+                    nc.tensor.matmul_mx(
+                        out=bank[:, s, c0 : c0 + P],
+                        lhsT=wd4_dealt[:, 2 * col0 : 2 * (col0 + P)].bitcast(FP4X4),
+                        lhsT_scale=wd_scale[:, N + col0 : N + col0 + P],
+                        rhs=h_codes[1][:, part].bitcast(FP8X4),
+                        rhs_scale=h_scales[1][:, part],
+                        start=(first and s == 0 and c0 == 0),
+                        stop=(not first and s == 1 and c0 + P == width),
+                    )
+
         def output_chunk(j0, width):
             places = slice(j0, j0 + width)
             y = ring3.tile([P, 4, width], F32, name="f32_stage")
-            per_bank = 512 // width
-            for t0 in range(0, 4, per_bank):
-                bank = psum.tile([P, per_bank, width], F32, name="gate_bank" if (t0 // per_bank) % 2 == 0 else "up_bank")
-                for t in range(t0, t0 + per_bank):
-                    nc.tensor.matmul_mx(
-                        out=bank[:, t - t0, :],
-                        lhsT=wd8_dealt[:, P * t : P * (t + 1)].bitcast(FP8X4),
-                        lhsT_scale=wd_scale[:, P * t : P * (t + 1)],
-                        rhs=h_codes[0][:, places].bitcast(FP8X4),
-                        rhs_scale=h_scales[0][:, places],
-                        start=(t == t0),
-                        stop=False,
-                    )
-                step = 512 if width == 512 else P
-                for t in range(t0, t0 + per_bank):
-                    for c0 in range(0, width, step):
-                        part = slice(j0 + c0, j0 + c0 + step)
-                        nc.tensor.matmul_mx(
-                            out=bank[:, t - t0, c0 : c0 + step],
-                            lhsT=wd4_dealt[:, 2 * P * t : 2 * P * (t + 1)].bitcast(FP4X4),
-                            lhsT_scale=wd_scale[:, N + P * t : N + P * (t + 1)],
-                            rhs=h_codes[1][:, part].bitcast(FP8X4),
-                            rhs_scale=h_scales[1][:, part],
-                            start=False,
-                            stop=(t == t0 + per_bank - 1 and c0 + step == width),
+            order = (wd4_passes, wd8_passes) if width == UNIT else (wd8_passes, wd4_passes)
+            for t0, tag in ((0, "gate_bank"), (2, "up_bank")):
+                bank = psum.tile([P, 2, width], F32, name=tag)
+                order[0](bank, t0, j0, width, True)
+                order[1](bank, t0, j0, width, False)
+                for s in range(2):
+                    t = t0 + s
+                    if j0 + width == J and t0 > 0:
+                        nc.vector.tensor_scalar(y[:, t, :], bank[:, s, :], bias[:, t : t + 1], None, ADD)
+                    else:
+                        nc.scalar.activation(
+                            out=y[:, t, :], in_=bank[:, s, :], func=IDENTITY, bias=bias[:, t : t + 1], scale=1.0
                         )
-                for t in range(t0, t0 + per_bank):
-                    nc.scalar.activation(
-                        out=y[:, t, :], in_=bank[:, t - t0, :], func=IDENTITY, bias=bias[:, t : t + 1], scale=1.0
-                    )
             nc.sync.dma_start(out=y_rows[:, :, places], in_=y[:])
             y_words = ring2.tile([P, 4 * width], BF16, name="y_words", align_bytes=64)
-            interleave(nc.vector.tensor_copy, y_words[:], y[:])
+            nc.vector.tensor_copy(out=as_words(y_words[:]), in_=as_planes(y[:]))
             nc.vector.quantize_mx(out=y_codes[:, places].bitcast(FP8X4), scales=y_scales[:, places], in_=y_words[:])
             nc.sync.dma_start(out=y_word_rows[:, places], in_=y_codes[:, places])
 
-        def store_scales(j0, width):
-            for q in range(4):
-                nc.sync.dma_start(
-                    out=out_2[0, 4 * q : 4 * q + 4, j0 : j0 + width].bitcast(I32),
-                    in_=y_scales[32 * q : 32 * q + 4, j0 : j0 + width].bitcast(I32),
-                )
-
-        hidden_unit(0, 0)
-        hidden_unit(0, 1)
-        deal_wu(1)
-        quantise_wg(0, 1, 0)
-        hidden_unit(0, 2)
-        quantise_wg(1, 1, 0)
-        hidden_unit(0, 3)
+        hidden_unit(0, 0, UNIT)
+        hidden_unit(0, UNIT, UNIT)
+        quantise_wg(0, 1, nc.scalar.copy, 4)
+        quantise_wg(1, 1, nc.vector.tensor_copy, 2)
+        hidden_unit(0, 2 * UNIT, UNIT)
         deal_wd()
-        hidden_unit(1, 0)
-        hidden_unit(1, 1)
-        hidden_unit(1, 2)
-        output_chunk(*OUT_CHUNKS[0])
-        hidden_unit(1, 3)
-        output_chunk(*OUT_CHUNKS[1])
-        store_scales(0, 768)
-        output_chunk(*OUT_CHUNKS[2])
-        output_chunk(*OUT_CHUNKS[3])
-        store_scales(768, 256)
+        hidden_unit(0, 3 * UNIT, UNIT)
+        chunks = [(j0, UNIT) for j0 in range(0, J - UNIT, UNIT)] + [(J - UNIT, P), (J - P, P)]
+        hidden_unit(1, *chunks[0])
+        for ahead, behind in zip(chunks[1:], chunks):
+            hidden_unit(1, *ahead)
+            output_chunk(*behind)
+        output_chunk(*chunks[-1])
+
+        for q in range(4):
+            queue = nc.sync if q % 2 else nc.scalar
+            queue.dma_start(
+                out=out_2[0, 4 * q : 4 * q + 4, :].bitcast(I32), in_=y_scales[32 * q : 32 * q + 4, :].bitcast(I32)
+            )

@@ -22,6 +22,7 @@ PASS = 512
 BANK = 512
 HALF = J // 2
 UNIT = 256
+WD8_ROW = 4
 
 
 def as_words(words):
@@ -49,7 +50,7 @@ def tile_list_gelu_mix_biasP_kernel(
         nc.sync.dma_start(offsets[:], offs)
 
         wu_scale_raw = kept("wu_scale_raw", [P, 2, R], U8)
-        wd_scale_raw = kept("wd_scale_raw", [P, 2, N], U8)
+        wd_scale_raw = kept("wd_scale_raw", [P, N], U8)
         nc.vector.memset(wu_scale_raw[:].bitcast(I32), 0)
         nc.vector.memset(wd_scale_raw[:].bitcast(I32), 0)
 
@@ -76,10 +77,10 @@ def tile_list_gelu_mix_biasP_kernel(
             nc.sync.dma_start(out=wu_raw[g][:].bitcast(I32), in_=cols.rearrange("a p c -> p a c").bitcast(I32))
 
         load_wu(0)
-        for q in range(4):
+        for row in range(4):
             nc.sync.dma_start(
-                out=wu_scale_raw[32 * q : 32 * q + 4, :, :].bitcast(I32),
-                in_=wu_scales[:, 4 * q : 4 * q + 4, :].rearrange("a q r -> q a r").bitcast(I32),
+                out=wu_scale_raw[row:P:32, :, :].bitcast(I32),
+                in_=wu_scales[:, row:16:4, :].rearrange("a q r -> q a r").bitcast(I32),
             )
         nc.sync.dma_start(out=place_w[0][:], in_=wgt[:, 0:HALF])
         load_plane(0, 0)
@@ -97,11 +98,10 @@ def tile_list_gelu_mix_biasP_kernel(
         nc.sync.dma_start(out=wd8_raw[:], in_=wd8_words[0].rearrange("p n i -> p (n i)").bitcast(I32))
         nc.sync.dma_start(out=wd4_raw[:].bitcast(I32), in_=wd4_words[0].bitcast(I32))
         nc.sync.dma_start(out=bias[:], in_=b.rearrange("(p t) -> p t", t=4))
-        for g, scales in enumerate((wd8_scales, wd4_scales)):
-            for q in range(4):
+        for row0, scales in ((WD8_ROW, wd8_scales), (0, wd4_scales)):
+            for row in range(4):
                 nc.sync.dma_start(
-                    out=wd_scale_raw[32 * q : 32 * q + 4, g, :].bitcast(I32),
-                    in_=scales[0, 4 * q : 4 * q + 4, :].bitcast(I32),
+                    out=wd_scale_raw[row0 + row : P : 32, :].bitcast(I32), in_=scales[0, row:16:4, :].bitcast(I32)
                 )
 
         x_codes = [kept("x_codes%d" % a, [P, J], I32) for a in range(2)]
@@ -111,7 +111,7 @@ def tile_list_gelu_mix_biasP_kernel(
         wu_scale = [kept("wu_scale%d" % g, [P, 2 * PASS], U8) for g in range(2)]
         wd8_dealt = kept("wd8_dealt", [P, N], I32)
         wd4_dealt = kept("wd4_dealt", [P, 2 * N], U8)
-        wd_scale = kept("wd_scale", [P, 2 * N], U8)
+        wd_scale = kept("wd_scale", [P, N], U8)
         picked = [[kept("picked%d%d" % (a, half), [P, 4, HALF], F32) for half in range(2)] for a in range(2)]
 
         def gather(a, i, j0, width):
@@ -161,8 +161,8 @@ def tile_list_gelu_mix_biasP_kernel(
                 in_=wd4_raw[:].bitcast(U16).rearrange("p (m t) -> p t m", t=4),
             )
             nc.vector.tensor_copy(
-                out=wd_scale[:].rearrange("p (g t m) -> p g t m", g=2, t=4),
-                in_=wd_scale_raw[:].rearrange("p g (m t) -> p g t m", t=4),
+                out=wd_scale[:].rearrange("p (t m) -> p t m", t=4),
+                in_=wd_scale_raw[:].rearrange("p (m t) -> p t m", t=4),
             )
 
         deal_wu(0)
@@ -239,7 +239,7 @@ def tile_list_gelu_mix_biasP_kernel(
                 nc.tensor.matmul_mx(
                     out=bank[:, s, :],
                     lhsT=wd8_dealt[:, cols].bitcast(FP8X4),
-                    lhsT_scale=wd_scale[:, cols],
+                    lhsT_scale=wd_scale[WD8_ROW:P, cols],
                     rhs=h_codes[0][:, j0 : j0 + width].bitcast(FP8X4),
                     rhs_scale=h_scales[0][:, j0 : j0 + width],
                     start=(first and s == 0),
@@ -254,7 +254,7 @@ def tile_list_gelu_mix_biasP_kernel(
                     nc.tensor.matmul_mx(
                         out=bank[:, s, c0 : c0 + P],
                         lhsT=wd4_dealt[:, 2 * col0 : 2 * (col0 + P)].bitcast(FP4X4),
-                        lhsT_scale=wd_scale[:, N + col0 : N + col0 + P],
+                        lhsT_scale=wd_scale[:, col0 : col0 + P],
                         rhs=h_codes[1][:, part].bitcast(FP8X4),
                         rhs_scale=h_scales[1][:, part],
                         start=(first and s == 0 and c0 == 0),
@@ -297,8 +297,6 @@ def tile_list_gelu_mix_biasP_kernel(
             output_chunk(*behind)
         output_chunk(*chunks[-1])
 
-        for q in range(4):
-            queue = nc.sync if q % 2 else nc.scalar
-            queue.dma_start(
-                out=out_2[0, 4 * q : 4 * q + 4, :].bitcast(I32), in_=y_scales[32 * q : 32 * q + 4, :].bitcast(I32)
-            )
+        for row in range(4):
+            queue = nc.sync if row % 2 else nc.scalar
+            queue.dma_start(out=out_2[0, row:16:4, :].bitcast(I32), in_=y_scales[row:P:32, :].bitcast(I32))

@@ -54,7 +54,8 @@ def tile_list_gelu_mix_biasP_kernel(
         nc.vector.memset(wu_scale_raw[:].bitcast(I32), 0)
         nc.vector.memset(wd_scale_raw[:].bitcast(I32), 0)
 
-        place_w = [kept("place_w%d" % half, [P, HALF], F32) for half in range(2)]
+        first_w = kept("first_w", [P, UNIT], F32)
+        other_w = kept("other_w", [P, J - UNIT], F32)
         x_planes = [[kept("x_plane%d%d" % (a, i), [P, T], F32) for i in range(4)] for a in range(2)]
         wu_raw = [kept("wu_raw%d" % g, [P, 2, 2 * PASS], U8) for g in range(2)]
         wd8_raw = kept("wd8_raw", [P, N], I32)
@@ -67,7 +68,7 @@ def tile_list_gelu_mix_biasP_kernel(
             nc.sync.dma_start(out=x_planes[a][i][:], in_=rows[:, i, :])
 
         def load_wg(a, g):
-            raw = ring3.tile([P, 4, PASS], F32, name="f32_stage")
+            raw = ring3.tile([P, 4, PASS], F32, name="f32_stage", bufs=4)
             rows = wg[a * PASS : (a + 1) * PASS, g * PASS : (g + 1) * PASS]
             nc.sync.dma_start(out=raw[:], in_=rows.rearrange("(p i) r -> p i r", i=4))
             wg_raw[(a, g)] = raw
@@ -76,16 +77,34 @@ def tile_list_gelu_mix_biasP_kernel(
             cols = wu_words[:, :, 2 * g * PASS : 2 * (g + 1) * PASS]
             nc.sync.dma_start(out=wu_raw[g][:].bitcast(I32), in_=cols.rearrange("a p c -> p a c").bitcast(I32))
 
+        def place_w(j0, j1):
+            return first_w[:, j0:j1] if j1 <= UNIT else other_w[:, j0 - UNIT : j1 - UNIT]
+
+        def load_place_w(j0, j1):
+            nc.sync.dma_start(out=place_w(j0, j1), in_=wgt[:, j0:j1])
+
+        def load_wu_scales():
+            for row in range(4):
+                nc.sync.dma_start(
+                    out=wu_scale_raw[row:P:32, :, :].bitcast(I32),
+                    in_=wu_scales[:, row:16:4, :].rearrange("a q r -> q a r").bitcast(I32),
+                )
+
+        def load_wd():
+            nc.sync.dma_start(out=wd8_raw[:], in_=wd8_words[0].rearrange("p n i -> p (n i)").bitcast(I32))
+            nc.sync.dma_start(out=wd4_raw[:].bitcast(I32), in_=wd4_words[0].bitcast(I32))
+            nc.sync.dma_start(out=bias[:], in_=b.rearrange("(p t) -> p t", t=4))
+            for row0, scales in ((WD8_ROW, wd8_scales), (0, wd4_scales)):
+                for row in range(4):
+                    nc.sync.dma_start(
+                        out=wd_scale_raw[row0 + row : P : 32, :].bitcast(I32), in_=scales[0, row:16:4, :].bitcast(I32)
+                    )
+
         load_wu(0)
-        for row in range(4):
-            nc.sync.dma_start(
-                out=wu_scale_raw[row:P:32, :, :].bitcast(I32),
-                in_=wu_scales[:, row:16:4, :].rearrange("a q r -> q a r").bitcast(I32),
-            )
-        nc.sync.dma_start(out=place_w[0][:], in_=wgt[:, 0:HALF])
+        load_wu_scales()
+        load_place_w(0, UNIT)
         load_plane(0, 0)
-        nc.sync.dma_start(out=place_w[1][:], in_=wgt[:, HALF:J])
-        load_wu(1)
+        load_place_w(UNIT, J)
         for i in range(1, 4):
             load_plane(0, i)
         for i in range(3):
@@ -95,14 +114,8 @@ def tile_list_gelu_mix_biasP_kernel(
         load_wg(1, 0)
         load_wg(1, 1)
         load_wg(0, 1)
-        nc.sync.dma_start(out=wd8_raw[:], in_=wd8_words[0].rearrange("p n i -> p (n i)").bitcast(I32))
-        nc.sync.dma_start(out=wd4_raw[:].bitcast(I32), in_=wd4_words[0].bitcast(I32))
-        nc.sync.dma_start(out=bias[:], in_=b.rearrange("(p t) -> p t", t=4))
-        for row0, scales in ((WD8_ROW, wd8_scales), (0, wd4_scales)):
-            for row in range(4):
-                nc.sync.dma_start(
-                    out=wd_scale_raw[row0 + row : P : 32, :].bitcast(I32), in_=scales[0, row:16:4, :].bitcast(I32)
-                )
+        load_wu(1)
+        load_wd()
 
         x_codes = [kept("x_codes%d" % a, [P, J], I32) for a in range(2)]
         x_scales = [kept("x_scales%d" % a, [P, J], U8) for a in range(2)]
@@ -112,34 +125,45 @@ def tile_list_gelu_mix_biasP_kernel(
         wd8_dealt = kept("wd8_dealt", [P, N], I32)
         wd4_dealt = kept("wd4_dealt", [P, 2 * N], U8)
         wd_scale = kept("wd_scale", [P, N], U8)
-        picked = [[kept("picked%d%d" % (a, half), [P, 4, HALF], F32) for half in range(2)] for a in range(2)]
+        picked = [kept("picked%d" % a, [P, 4, J], F32) for a in range(2)]
+        x_words = [kept("x_words%d" % a, [P, 4 * J], BF16) for a in range(2)]
 
         def gather(a, i, j0, width):
-            half, c0 = divmod(j0, HALF)
             nc.vector.tensor_tensor(
-                picked[a][half][:, i, c0 : c0 + width],
+                picked[a][:, i, j0 : j0 + width],
                 x_planes[a][i][:].indirect(offsets[:, j0 // 16 : (j0 + width) // 16]),
-                place_w[half][:, c0 : c0 + width],
+                place_w(j0, j0 + width),
                 MULT,
             )
 
-        def quantise_x(a, j0, width):
-            half, c0 = divmod(j0, HALF)
-            words = ring3.tile([P, 4 * width], BF16, name="x_words", align_bytes=64)
-            nc.scalar.copy(out=as_words(words[:]), in_=as_planes(picked[a][half][:, :, c0 : c0 + width]))
-            places = slice(j0, j0 + width)
-            nc.vector.quantize_mx(out=x_codes[a][:, places].bitcast(FP8X4), scales=x_scales[a][:, places], in_=words[:])
+        def round_x(copy, a, i0, planes, j0, width):
+            words = as_words(x_words[a][:, 4 * j0 : 4 * (j0 + width)])
+            copy(out=words[:, :, i0 : i0 + planes, :], in_=as_planes(picked[a][:, i0 : i0 + planes, j0 : j0 + width]))
 
-        def quantise_wg(a, g, copy, pieces):
+        def quantise_x(a, j0, width):
+            places = slice(j0, j0 + width)
+            nc.vector.quantize_mx(
+                out=x_codes[a][:, places].bitcast(FP8X4),
+                scales=x_scales[a][:, places],
+                in_=x_words[a][:, 4 * j0 : 4 * (j0 + width)],
+            )
+
+        def quantise_wg(a, g, copies, split):
             words = ring2.tile([P, 4 * PASS], BF16, name="wg_words", align_bytes=64)
             dealt = words[:].rearrange("p (u e m i) -> p u m i e", u=2, e=2, i=4)
             raw = wg_raw[(a, g)][:].rearrange("p i (m u e) -> p u m i e", u=2, e=2)
-            step = P // pieces
-            for m0 in range(0, P, step):
-                copy(out=dealt[:, :, m0 : m0 + step], in_=raw[:, :, m0 : m0 + step])
-            wg_codes[(a, g)] = kept("wg_codes%d%d" % (a, g), [P, PASS], I32)
-            wg_scales[(a, g)] = kept("wg_scales%d%d" % (a, g), [P, PASS], U8)
-            nc.vector.quantize_mx(out=wg_codes[(a, g)][:].bitcast(FP8X4), scales=wg_scales[(a, g)][:], in_=words[:])
+            codes = wg_codes[(a, g)] = kept("wg_codes%d%d" % (a, g), [P, PASS], I32)
+            scales = wg_scales[(a, g)] = kept("first_w" if (a, g) == (0, 0) else "wg_scales%d%d" % (a, g), [P, PASS], U8)
+            halves = 1 if split else 2
+            for u in range(0, 2, halves):
+                step = P // len(copies)
+                for m0 in range(0, P, step):
+                    copy = copies[m0 // step]
+                    copy(out=dealt[:, u : u + halves, m0 : m0 + step], in_=raw[:, u : u + halves, m0 : m0 + step])
+                c0, c1 = 2 * P * u, 2 * P * (u + halves)
+                nc.vector.quantize_mx(
+                    out=codes[:, c0:c1].bitcast(FP8X4), scales=scales[:, c0:c1], in_=words[:, 4 * c0 : 4 * c1]
+                )
 
         def deal_wu(g):
             nc.vector.tensor_copy(
@@ -165,28 +189,40 @@ def tile_list_gelu_mix_biasP_kernel(
                 in_=wd_scale_raw[:].rearrange("p (m t) -> p t m", t=4),
             )
 
+        on_scalar, on_vector = nc.scalar.copy, nc.vector.tensor_copy
+        table_warm_up = kept("table_warm_up", [P, 1], F32)
+        nc.scalar.activation(out=table_warm_up[:], in_=first_w[:, 0:1], func=GELU)
+
         deal_wu(0)
-        deal_wu(1)
-        for i in range(4):
-            for j0 in range(0, J, HALF):
-                gather(0, i, j0, HALF)
-        for j0 in range(0, J, HALF):
-            quantise_x(0, j0, HALF)
-        quantise_wg(0, 0, nc.scalar.copy, 1)
         for i in range(3):
-            for j0 in range(0, J, HALF):
-                gather(1, i, j0, HALF)
-        quantise_wg(1, 0, nc.vector.tensor_copy, 2)
-        for j0 in range(0, J, UNIT):
-            gather(1, 3, j0, UNIT)
-            quantise_x(1, j0, UNIT)
+            gather(0, i, 0, UNIT)
+            gather(0, i, UNIT, J - UNIT)
+        for j0, width in ((0, UNIT), (UNIT, UNIT), (HALF, HALF)):
+            gather(0, 3, j0, width)
+        for j0 in range(0, J, HALF):
+            round_x(on_scalar, 0, 0, 4, j0, HALF)
+            quantise_x(0, j0, HALF)
+        for i in range(3):
+            gather(1, i, 0, UNIT)
+            gather(1, i, UNIT, J - UNIT)
+        units = [(j0, UNIT) for j0 in range(0, J, UNIT)]
+        for j0, width in units:
+            gather(1, 3, j0, width)
+            round_x(on_scalar, 1, 0, 4, j0, width)
+            quantise_x(1, j0, width)
+            if j0 == 0:
+                quantise_wg(0, 0, [on_scalar], False)
+            if j0 == 0:
+                quantise_wg(1, 0, [on_vector], True)
 
         h_codes = [kept("h_codes%d" % g, [P, J], I32) for g in range(2)]
         h_scales = [kept("h_scales%d" % g, [P, J], U8) for g in range(2)]
+        h_words = [kept(name, [P, 4 * J], BF16) for name in ("h_words0", "x_words0")]
+        gates, sums = {}, {}
         y_codes = kept("y_codes", [P, J], I32)
         y_scales = kept("y_scales", [P, J], U8)
 
-        def hidden_unit(g, j0, width):
+        def gate_unit(g, j0, width):
             passes = (0, 1) if g == 0 and j0 < 2 * UNIT else (1, 0)
             places = slice(j0, j0 + width)
             gated = ring3.tile([P, 4, width], F32, name="gated")
@@ -206,7 +242,11 @@ def tile_list_gelu_mix_biasP_kernel(
                             stop=(a == passes[1] and s == per_bank - 1),
                         )
                 nc.scalar.activation(out=gated[:, t0 : t0 + per_bank, :], in_=bank[:], func=GELU)
-            h_words = ring3.tile([P, 4 * width], BF16, name="h_words", align_bytes=64)
+            gates[(g, j0)] = gated
+
+        def up_unit(g, j0, width):
+            passes = (0, 1) if g == 0 and j0 < 2 * UNIT else (1, 0)
+            gated = gates[(g, j0)]
             for c0 in range(0, width, P):
                 bank = psum.tile([P, 4, P], F32, name="up_bank")
                 part = slice(j0 + c0, j0 + c0 + P)
@@ -223,12 +263,23 @@ def tile_list_gelu_mix_biasP_kernel(
                             stop=(a == passes[1] and t == 3),
                         )
                 nc.vector.tensor_tensor(
-                    as_words(h_words[:, 4 * c0 : 4 * (c0 + P)]),
+                    as_words(h_words[g][:, 4 * (j0 + c0) : 4 * (j0 + c0 + P)]),
                     as_planes(bank[:]),
                     as_planes(gated[:, :, c0 : c0 + P]),
                     MULT,
                 )
-            nc.vector.quantize_mx(out=h_codes[g][:, places].bitcast(FP8X4), scales=h_scales[g][:, places], in_=h_words[:])
+
+        def hidden_unit(g, j0, width):
+            gate_unit(g, j0, width)
+            up_unit(g, j0, width)
+
+        def quantise_h(g, j0, width):
+            places = slice(j0, j0 + width)
+            nc.vector.quantize_mx(
+                out=h_codes[g][:, places].bitcast(FP8X4),
+                scales=h_scales[g][:, places],
+                in_=h_words[g][:, 4 * j0 : 4 * (j0 + width)],
+            )
 
         y_rows = out_0.rearrange("(p t) j -> p t j", t=4)
         y_word_rows = out_1[0].rearrange("p j i -> p (j i)").bitcast(I32)
@@ -261,41 +312,75 @@ def tile_list_gelu_mix_biasP_kernel(
                         stop=(not first and s == 1 and c0 + P == width),
                     )
 
-        def output_chunk(j0, width):
+        def output_bank(j0, width, t0, on_vector_engine=False, store=2):
             places = slice(j0, j0 + width)
-            y = ring3.tile([P, 4, width], F32, name="f32_stage")
+            if t0 == 0:
+                sums[j0] = ring3.tile([P, 4, width], F32, name="f32_stage", bufs=4)
+            y = sums[j0]
             order = (wd4_passes, wd8_passes) if width == UNIT else (wd8_passes, wd4_passes)
-            for t0, tag in ((0, "gate_bank"), (2, "up_bank")):
-                bank = psum.tile([P, 2, width], F32, name=tag)
-                order[0](bank, t0, j0, width, True)
-                order[1](bank, t0, j0, width, False)
-                for s in range(2):
-                    t = t0 + s
-                    if j0 + width == J and t0 > 0:
-                        nc.vector.tensor_scalar(y[:, t, :], bank[:, s, :], bias[:, t : t + 1], None, ADD)
-                    else:
-                        nc.scalar.activation(
-                            out=y[:, t, :], in_=bank[:, s, :], func=IDENTITY, bias=bias[:, t : t + 1], scale=1.0
-                        )
-            nc.sync.dma_start(out=y_rows[:, :, places], in_=y[:])
+            bank = psum.tile([P, 2, width], F32, name="up_bank" if t0 else "gate_bank")
+            order[0](bank, t0, j0, width, True)
+            order[1](bank, t0, j0, width, False)
+            if on_vector_engine:
+                spread = bias[:, t0 : t0 + 2].unsqueeze(2).to_broadcast([P, 2, width])
+                nc.vector.tensor_tensor(y[:, t0 : t0 + 2, :], bank[:], spread, ADD)
+            else:
+                for t in (t0, t0 + 1):
+                    nc.scalar.activation(
+                        out=y[:, t, :], in_=bank[:, t - t0, :], func=IDENTITY, bias=bias[:, t : t + 1], scale=1.0
+                    )
+            if store:
+                rows = slice(t0 + 2 - store, t0 + 2)
+                nc.sync.dma_start(out=y_rows[:, rows, places], in_=y[:, rows, :])
+
+        def output_sums(j0, width, vector_banks=()):
+            output_bank(j0, width, 0, 0 in vector_banks, 0)
+            output_bank(j0, width, 2, 2 in vector_banks, 4)
+
+        def output_codes(j0, width, copy):
+            places = slice(j0, j0 + width)
+            y = sums[j0]
             y_words = ring2.tile([P, 4 * width], BF16, name="y_words", align_bytes=64)
-            nc.vector.tensor_copy(out=as_words(y_words[:]), in_=as_planes(y[:]))
+            copy(out=as_words(y_words[:]), in_=as_planes(y[:]))
             nc.vector.quantize_mx(out=y_codes[:, places].bitcast(FP8X4), scales=y_scales[:, places], in_=y_words[:])
             nc.sync.dma_start(out=y_word_rows[:, places], in_=y_codes[:, places])
 
-        hidden_unit(0, 0, UNIT)
-        hidden_unit(0, UNIT, UNIT)
-        quantise_wg(0, 1, nc.scalar.copy, 4)
-        quantise_wg(1, 1, nc.vector.tensor_copy, 2)
-        hidden_unit(0, 2 * UNIT, UNIT)
+        for unit in units[:2]:
+            hidden_unit(0, *unit)
+        quantise_wg(1, 1, [on_vector]*2, False)
+        quantise_wg(0, 1, [on_scalar]*4, False)
+        deal_wu(1)
+        for unit in units[2:]:
+            hidden_unit(0, *unit)
+        hidden_unit(1, 0, 256)
+        quantise_h(1, 0, 256)
         deal_wd()
-        hidden_unit(0, 3 * UNIT, UNIT)
-        chunks = [(j0, UNIT) for j0 in range(0, J - UNIT, UNIT)] + [(J - UNIT, P), (J - P, P)]
-        hidden_unit(1, *chunks[0])
-        for ahead, behind in zip(chunks[1:], chunks):
-            hidden_unit(1, *ahead)
-            output_chunk(*behind)
-        output_chunk(*chunks[-1])
+        quantise_h(0, 0, 256)
+        hidden_unit(1, 256, 256)
+        quantise_h(1, 256, 256)
+        quantise_h(0, 256, 256)
+        gate_unit(1, 512, 256)
+        output_sums(0, 256, ())
+        up_unit(1, 512, 256)
+        quantise_h(1, 512, 256)
+        output_codes(0, 256, on_vector)
+        quantise_h(0, 512, 512)
+        gate_unit(1, 768, 128)
+        output_sums(256, 256, ())
+        up_unit(1, 768, 128)
+        quantise_h(1, 768, 128)
+        output_codes(256, 256, on_vector)
+        gate_unit(1, 896, 128)
+        output_sums(512, 128, ())
+        up_unit(1, 896, 128)
+        quantise_h(1, 896, 128)
+        output_codes(512, 128, on_vector)
+        output_sums(640, 128, ())
+        output_sums(768, 128, ())
+        output_codes(640, 128, on_vector)
+        output_sums(896, 128, (2,))
+        output_codes(768, 128, on_vector)
+        output_codes(896, 128, on_vector)
 
         for row in range(4):
             queue = nc.sync if row % 2 else nc.scalar

@@ -153,7 +153,6 @@ def tile_list_gelu_mix_biasP_kernel(
             dealt = words[:].rearrange("p (u e m i) -> p u m i e", u=2, e=2, i=4)
             raw = wg_raw[(a, g)][:].rearrange("p i (m u e) -> p u m i e", u=2, e=2)
             codes = wg_codes[(a, g)] = kept("wg_codes%d%d" % (a, g), [P, PASS], I32)
-            scales = wg_scales[(a, g)] = kept("first_w" if (a, g) == (0, 0) else "wg_scales%d%d" % (a, g), [P, PASS], U8)
             halves = 1 if split else 2
             for u in range(0, 2, halves):
                 step = P // len(copies)
@@ -161,9 +160,13 @@ def tile_list_gelu_mix_biasP_kernel(
                     copy = copies[m0 // step]
                     copy(out=dealt[:, u : u + halves, m0 : m0 + step], in_=raw[:, u : u + halves, m0 : m0 + step])
                 c0, c1 = 2 * P * u, 2 * P * (u + halves)
+                name = "first_w" if (a, g, u) == (0, 0, 1) else "wg_scales%d%d%d" % (a, g, u)
+                scales = kept(name, [P, c1 - c0], U8)
                 nc.vector.quantize_mx(
-                    out=codes[:, c0:c1].bitcast(FP8X4), scales=scales[:, c0:c1], in_=words[:, 4 * c0 : 4 * c1]
+                    out=codes[:, c0:c1].bitcast(FP8X4), scales=scales[:], in_=words[:, 4 * c0 : 4 * c1]
                 )
+                for t in range(2 * u, 2 * (u + halves)):
+                    wg_scales[(a, g, t)] = scales[:, P * t - c0 : P * (t + 1) - c0]
 
         def deal_wu(g):
             nc.vector.tensor_copy(
@@ -211,8 +214,8 @@ def tile_list_gelu_mix_biasP_kernel(
             round_x(on_scalar, 1, 0, 4, j0, width)
             quantise_x(1, j0, width)
             if j0 == 0:
-                quantise_wg(0, 0, [on_scalar], False)
-            if j0 == 0:
+                quantise_wg(0, 0, [on_scalar], True)
+            if j0 == UNIT:
                 quantise_wg(1, 0, [on_vector], True)
 
         h_codes = [kept("h_codes%d" % g, [P, J], I32) for g in range(2)]
@@ -235,7 +238,7 @@ def tile_list_gelu_mix_biasP_kernel(
                         nc.tensor.matmul_mx(
                             out=bank[:, s, :],
                             lhsT=wg_codes[(a, g)][:, cols].bitcast(FP8X4),
-                            lhsT_scale=wg_scales[(a, g)][:, cols],
+                            lhsT_scale=wg_scales[(a, g, t0 + s)],
                             rhs=x_codes[a][:, places].bitcast(FP8X4),
                             rhs_scale=x_scales[a][:, places],
                             start=(a == passes[0] and s == 0),
@@ -337,18 +340,20 @@ def tile_list_gelu_mix_biasP_kernel(
             output_bank(j0, width, 0, 0 in vector_banks, 0)
             output_bank(j0, width, 2, 2 in vector_banks, 4)
 
-        def output_codes(j0, width, copy):
+        def output_codes(j0, width, copy, stored):
             places = slice(j0, j0 + width)
             y = sums[j0]
             y_words = ring2.tile([P, 4 * width], BF16, name="y_words", align_bytes=64)
             copy(out=as_words(y_words[:]), in_=as_planes(y[:]))
             nc.vector.quantize_mx(out=y_codes[:, places].bitcast(FP8X4), scales=y_scales[:, places], in_=y_words[:])
-            nc.sync.dma_start(out=y_word_rows[:, places], in_=y_codes[:, places])
+            if stored:
+                done = slice(j0 + width - stored, j0 + width)
+                nc.sync.dma_start(out=y_word_rows[:, done], in_=y_codes[:, done])
 
         for unit in units[:2]:
             hidden_unit(0, *unit)
         quantise_wg(1, 1, [on_vector]*2, False)
-        quantise_wg(0, 1, [on_scalar]*4, False)
+        quantise_wg(0, 1, [on_scalar]*2, True)
         deal_wu(1)
         for unit in units[2:]:
             hidden_unit(0, *unit)
@@ -363,24 +368,24 @@ def tile_list_gelu_mix_biasP_kernel(
         output_sums(0, 256, ())
         up_unit(1, 512, 256)
         quantise_h(1, 512, 256)
-        output_codes(0, 256, on_vector)
+        output_codes(0, 256, on_vector, 256)
         quantise_h(0, 512, 512)
         gate_unit(1, 768, 128)
         output_sums(256, 256, ())
         up_unit(1, 768, 128)
         quantise_h(1, 768, 128)
-        output_codes(256, 256, on_vector)
+        output_codes(256, 256, on_vector, 256)
         gate_unit(1, 896, 128)
         output_sums(512, 128, ())
         up_unit(1, 896, 128)
         quantise_h(1, 896, 128)
-        output_codes(512, 128, on_vector)
+        output_codes(512, 128, on_vector, 0)
         output_sums(640, 128, ())
         output_sums(768, 128, ())
-        output_codes(640, 128, on_vector)
+        output_codes(640, 128, on_vector, 256)
         output_sums(896, 128, (2,))
-        output_codes(768, 128, on_vector)
-        output_codes(896, 128, on_vector)
+        output_codes(768, 128, on_vector, 0)
+        output_codes(896, 128, on_vector, 256)
 
         for row in range(4):
             queue = nc.sync if row % 2 else nc.scalar

@@ -1,6 +1,7 @@
 from contextlib import ExitStack
 
 import concourse.mybir as mybir
+from concourse.masks import make_identity
 
 K, R, N, T, J = 1024, 1024, 512, 2048, 1024
 FLOPS = 2 * J * (2 * K * R + R * N)
@@ -22,6 +23,7 @@ PASS = 512
 BANK = 512
 HALF = J // 2
 UNIT = 256
+LAST = J - UNIT
 WD8_ROW = 4
 
 
@@ -47,7 +49,6 @@ def tile_list_gelu_mix_biasP_kernel(
             return keep.tile(shape, dtype, name=name, align_bytes=64)
 
         offsets = keep.tile([P, J // 16], U16, name="offsets")
-        nc.sync.dma_start(offsets[:], offs)
 
         wu_scale_raw = kept("wu_scale_raw", [P, 2, R], U8)
         wd_scale_raw = kept("wd_scale_raw", [P, N], U8)
@@ -55,7 +56,7 @@ def tile_list_gelu_mix_biasP_kernel(
         nc.vector.memset(wd_scale_raw[:].bitcast(I32), 0)
 
         first_w = kept("first_w", [P, UNIT], F32)
-        other_w = kept("other_w", [P, J - UNIT], F32)
+        weights = kept("weights", [P, J], F32)
         x_planes = [[kept("x_plane%d%d" % (a, i), [P, T], F32) for i in range(4)] for a in range(2)]
         wu_raw = [kept("wu_raw%d" % g, [P, 2, 2 * PASS], U8) for g in range(2)]
         wd8_raw = kept("wd8_raw", [P, N], I32)
@@ -78,10 +79,20 @@ def tile_list_gelu_mix_biasP_kernel(
             nc.sync.dma_start(out=wu_raw[g][:].bitcast(I32), in_=cols.rearrange("a p c -> p a c").bitcast(I32))
 
         def place_w(j0, j1):
-            return first_w[:, j0:j1] if j1 <= UNIT else other_w[:, j0 - UNIT : j1 - UNIT]
+            return first_w[:, j0:j1] if j1 <= UNIT else weights[:, j0:j1]
 
-        def load_place_w(j0, j1):
-            nc.sync.dma_start(out=place_w(j0, j1), in_=wgt[:, j0:j1])
+        def spread_weights():
+            turned = psum.tile([P, P], F32, name="up_bank")
+            nc.tensor.transpose(turned[:], w_rows[:], identity[:])
+            by_block = turned[:].rearrange("k (r jb) -> k jb r", jb=4)
+            nc.scalar.copy(out=w_spread[:], in_=by_block.unsqueeze(3).to_broadcast([P, 4, 32, 4]))
+            bank = psum.tile([P, HALF], F32, name="gate_bank")
+            for jb in range(4):
+                nc.tensor.transpose(
+                    bank[:, jb * P : (jb + 1) * P], w_spread[:, jb].rearrange("k r d -> k (r d)"), identity[:]
+                )
+            nc.scalar.copy(out=weights[:, 0:HALF], in_=bank[:])
+            nc.scalar.copy(out=first_w[:], in_=bank[:, 0:UNIT])
 
         def load_wu_scales():
             for row in range(4):
@@ -100,11 +111,16 @@ def tile_list_gelu_mix_biasP_kernel(
                         out=wd_scale_raw[row0 + row : P : 32, :].bitcast(I32), in_=scales[0, row:16:4, :].bitcast(I32)
                     )
 
+        w_rows = kept("wg_codes00", [P, P], F32)
+        w_spread = kept("wg_codes10", [P, 4, 32, 4], F32)
+        identity = kept("wg_codes01", [P, P], F32)
+        make_identity(nc, identity[:])
+        nc.sync.dma_start(out=w_rows[:], in_=wgt[0:P:4, 0:HALF].rearrange("r (jb k) -> r jb k", k=P))
         load_wu(0)
+        nc.sync.dma_start(out=weights[:, HALF:J], in_=wgt[:, HALF:J])
         load_wu_scales()
-        load_place_w(0, UNIT)
         load_plane(0, 0)
-        load_place_w(UNIT, J)
+        nc.sync.dma_start(offsets[:], offs)
         for i in range(1, 4):
             load_plane(0, i)
         for i in range(3):
@@ -194,23 +210,25 @@ def tile_list_gelu_mix_biasP_kernel(
 
         on_scalar, on_vector = nc.scalar.copy, nc.vector.tensor_copy
         table_warm_up = kept("table_warm_up", [P, 1], F32)
-        nc.scalar.activation(out=table_warm_up[:], in_=first_w[:, 0:1], func=GELU)
+        nc.scalar.activation(out=table_warm_up[:], in_=identity[:, 0:1], func=GELU)
+        spread_weights()
 
         deal_wu(0)
-        for i in range(3):
-            gather(0, i, 0, UNIT)
-            gather(0, i, UNIT, J - UNIT)
-        for j0, width in ((0, UNIT), (UNIT, UNIT), (HALF, HALF)):
-            gather(0, 3, j0, width)
+        gather(0, 0, HALF, HALF)
+        gather(0, 0, 0, HALF)
+        for i in (1, 2):
+            gather(0, i, 0, J)
+        for j0 in (0, HALF):
+            gather(0, 3, j0, HALF)
         for j0 in range(0, J, HALF):
             round_x(on_scalar, 0, 0, 4, j0, HALF)
             quantise_x(0, j0, HALF)
         for i in range(3):
-            gather(1, i, 0, UNIT)
-            gather(1, i, UNIT, J - UNIT)
+            gather(1, i, 0, J)
         units = [(j0, UNIT) for j0 in range(0, J, UNIT)]
         for j0, width in units:
-            gather(1, 3, j0, width)
+            if j0 < LAST:
+                gather(1, 3, j0, width if j0 < HALF else HALF)
             round_x(on_scalar, 1, 0, 4, j0, width)
             quantise_x(1, j0, width)
             if j0 == 0:
@@ -225,52 +243,72 @@ def tile_list_gelu_mix_biasP_kernel(
         y_codes = kept("y_codes", [P, J], I32)
         y_scales = kept("y_scales", [P, J], U8)
 
-        def gate_unit(g, j0, width):
-            passes = (0, 1) if g == 0 and j0 < 2 * UNIT else (1, 0)
-            places = slice(j0, j0 + width)
-            gated = ring3.tile([P, 4, width], F32, name="gated")
+        gate_banks, up_banks = {}, {}
+
+        def pass_order(g, j0):
+            return (0, 1) if g == 0 and j0 < 2 * UNIT else (1, 0)
+
+        def gate_pass(g, j0, width, step, t0):
             per_bank = BANK // width
-            for t0 in range(0, 4, per_bank):
-                bank = psum.tile([P, per_bank, width], F32, name="gate_bank")
-                for a in passes:
-                    for s in range(per_bank):
-                        cols = slice(P * (t0 + s), P * (t0 + s + 1))
-                        nc.tensor.matmul_mx(
-                            out=bank[:, s, :],
-                            lhsT=wg_codes[(a, g)][:, cols].bitcast(FP8X4),
-                            lhsT_scale=wg_scales[(a, g, t0 + s)],
-                            rhs=x_codes[a][:, places].bitcast(FP8X4),
-                            rhs_scale=x_scales[a][:, places],
-                            start=(a == passes[0] and s == 0),
-                            stop=(a == passes[1] and s == per_bank - 1),
-                        )
-                nc.scalar.activation(out=gated[:, t0 : t0 + per_bank, :], in_=bank[:], func=GELU)
-            gates[(g, j0)] = gated
+            a = pass_order(g, j0)[step]
+            places = slice(j0, j0 + width)
+            if step == 0:
+                gate_banks[(g, j0, t0)] = psum.tile([P, per_bank, width], F32, name="gate_bank")
+            bank = gate_banks[(g, j0, t0)]
+            for s in range(per_bank):
+                cols = slice(P * (t0 + s), P * (t0 + s + 1))
+                nc.tensor.matmul_mx(
+                    out=bank[:, s, :],
+                    lhsT=wg_codes[(a, g)][:, cols].bitcast(FP8X4),
+                    lhsT_scale=wg_scales[(a, g, t0 + s)],
+                    rhs=x_codes[a][:, places].bitcast(FP8X4),
+                    rhs_scale=x_scales[a][:, places],
+                    start=(step == 0 and s == 0),
+                    stop=(step == 1 and s == per_bank - 1),
+                )
+            if step == 1:
+                if t0 == 0:
+                    gates[(g, j0)] = ring3.tile([P, 4, width], F32, name="gated")
+                nc.scalar.activation(out=gates[(g, j0)][:, t0 : t0 + per_bank, :], in_=bank[:], func=GELU)
+
+        def gate_step(g, j0, width, step):
+            for t0 in range(0, 4, BANK // width):
+                gate_pass(g, j0, width, step, t0)
+
+        def gate_unit(g, j0, width):
+            for t0 in range(0, 4, BANK // width):
+                for step in range(2):
+                    gate_pass(g, j0, width, step, t0)
+
+        def up_passes(g, j0):
+            passes = pass_order(g, j0)
+            bank = up_banks[(g, j0)] = psum.tile([P, 4, P], F32, name="up_bank")
+            part = slice(j0, j0 + P)
+            for a in passes:
+                for t in range(4):
+                    col0 = PASS * a + P * t
+                    nc.tensor.matmul_mx(
+                        out=bank[:, t, :],
+                        lhsT=wu_dealt[g][:, 2 * col0 : 2 * (col0 + P)].bitcast(FP4X4),
+                        lhsT_scale=wu_scale[g][:, col0 : col0 + P],
+                        rhs=x_codes[a][:, part].bitcast(FP8X4),
+                        rhs_scale=x_scales[a][:, part],
+                        start=(a == passes[0] and t == 0),
+                        stop=(a == passes[1] and t == 3),
+                    )
+
+        def product(g, j0, c0):
+            nc.vector.tensor_tensor(
+                as_words(h_words[g][:, 4 * (j0 + c0) : 4 * (j0 + c0 + P)]),
+                as_planes(up_banks[(g, j0 + c0)][:]),
+                as_planes(gates[(g, j0)][:, :, c0 : c0 + P]),
+                MULT,
+            )
 
         def up_unit(g, j0, width):
-            passes = (0, 1) if g == 0 and j0 < 2 * UNIT else (1, 0)
-            gated = gates[(g, j0)]
             for c0 in range(0, width, P):
-                bank = psum.tile([P, 4, P], F32, name="up_bank")
-                part = slice(j0 + c0, j0 + c0 + P)
-                for a in passes:
-                    for t in range(4):
-                        col0 = PASS * a + P * t
-                        nc.tensor.matmul_mx(
-                            out=bank[:, t, :],
-                            lhsT=wu_dealt[g][:, 2 * col0 : 2 * (col0 + P)].bitcast(FP4X4),
-                            lhsT_scale=wu_scale[g][:, col0 : col0 + P],
-                            rhs=x_codes[a][:, part].bitcast(FP8X4),
-                            rhs_scale=x_scales[a][:, part],
-                            start=(a == passes[0] and t == 0),
-                            stop=(a == passes[1] and t == 3),
-                        )
-                nc.vector.tensor_tensor(
-                    as_words(h_words[g][:, 4 * (j0 + c0) : 4 * (j0 + c0 + P)]),
-                    as_planes(bank[:]),
-                    as_planes(gated[:, :, c0 : c0 + P]),
-                    MULT,
-                )
+                up_passes(g, j0 + c0)
+                product(g, j0, c0)
 
         def hidden_unit(g, j0, width):
             gate_unit(g, j0, width)
@@ -352,18 +390,17 @@ def tile_list_gelu_mix_biasP_kernel(
 
         for unit in units[:2]:
             hidden_unit(0, *unit)
-        quantise_wg(1, 1, [on_vector]*2, False)
-        quantise_wg(0, 1, [on_scalar]*2, True)
+        quantise_wg(1, 1, [on_vector], False)
+        quantise_wg(0, 1, [on_scalar], True)
         deal_wu(1)
         for unit in units[2:]:
             hidden_unit(0, *unit)
         hidden_unit(1, 0, 256)
         quantise_h(1, 0, 256)
         deal_wd()
-        quantise_h(0, 0, 256)
+        quantise_h(0, 0, 512)
         hidden_unit(1, 256, 256)
         quantise_h(1, 256, 256)
-        quantise_h(0, 256, 256)
         gate_unit(1, 512, 256)
         output_sums(0, 256, ())
         up_unit(1, 512, 256)

@@ -280,22 +280,24 @@ def tile_list_gelu_mix_biasP_kernel(
                 for step in range(2):
                     gate_pass(g, j0, width, step, t0)
 
-        def up_passes(g, j0):
+        def up_passes(g, j0, width):
             passes = pass_order(g, j0)
-            bank = up_banks[(g, j0)] = psum.tile([P, 4, P], F32, name="up_bank")
-            part = slice(j0, j0 + P)
+            starts = range(j0, j0 + width, P)
+            for j1 in starts:
+                up_banks[(g, j1)] = psum.tile([P, 4, P], F32, name="up_bank")
             for a in passes:
                 for t in range(4):
                     col0 = PASS * a + P * t
-                    nc.tensor.matmul_mx(
-                        out=bank[:, t, :],
-                        lhsT=wu_dealt[g][:, 2 * col0 : 2 * (col0 + P)].bitcast(FP4X4),
-                        lhsT_scale=wu_scale[g][:, col0 : col0 + P],
-                        rhs=x_codes[a][:, part].bitcast(FP8X4),
-                        rhs_scale=x_scales[a][:, part],
-                        start=(a == passes[0] and t == 0),
-                        stop=(a == passes[1] and t == 3),
-                    )
+                    for j1 in starts:
+                        nc.tensor.matmul_mx(
+                            out=up_banks[(g, j1)][:, t, :],
+                            lhsT=wu_dealt[g][:, 2 * col0 : 2 * (col0 + P)].bitcast(FP4X4),
+                            lhsT_scale=wu_scale[g][:, col0 : col0 + P],
+                            rhs=x_codes[a][:, j1 : j1 + P].bitcast(FP8X4),
+                            rhs_scale=x_scales[a][:, j1 : j1 + P],
+                            start=(a == passes[0] and t == 0),
+                            stop=(a == passes[1] and t == 3),
+                        )
 
         def product(g, j0, c0):
             nc.vector.tensor_tensor(
@@ -306,8 +308,8 @@ def tile_list_gelu_mix_biasP_kernel(
             )
 
         def up_unit(g, j0, width):
+            up_passes(g, j0, width)
             for c0 in range(0, width, P):
-                up_passes(g, j0 + c0)
                 product(g, j0, c0)
 
         def hidden_unit(g, j0, width):

@@ -28,11 +28,11 @@ WD8_ROW = 4
 
 
 def as_words(words):
-    return words.rearrange("p (c e t) -> p c t e", e=2, t=4)
+    return words.rearrange("p (c e t) -> p c t e", e=4, t=4)
 
 
 def as_planes(planes):
-    return planes.rearrange("p t (c e) -> p c t e", e=2)
+    return planes.rearrange("p t (c e) -> p c t e", e=4)
 
 
 def tile_list_gelu_mix_biasP_kernel(
@@ -174,7 +174,13 @@ def tile_list_gelu_mix_biasP_kernel(
                 step = P // len(copies)
                 for m0 in range(0, P, step):
                     copy = copies[m0 // step]
-                    copy(out=dealt[:, u : u + halves, m0 : m0 + step], in_=raw[:, u : u + halves, m0 : m0 + step])
+                    if split:
+                        copy(out=dealt[:, u, m0 : m0 + step], in_=raw[:, u, m0 : m0 + step])
+                    else:
+                        copy(
+                            out=words[:].rearrange("p (t m i) -> p m i t", t=4, i=4),
+                            in_=wg_raw[(a, g)][:].rearrange("p i (m t) -> p m i t", t=4),
+                        )
                 c0, c1 = 2 * P * u, 2 * P * (u + halves)
                 name = "first_w" if (a, g, u) == (0, 0, 1) else "wg_scales%d%d%d" % (a, g, u)
                 scales = kept(name, [P, c1 - c0], U8)
@@ -268,8 +274,10 @@ def tile_list_gelu_mix_biasP_kernel(
                 )
             if step == 1:
                 if t0 == 0:
-                    gates[(g, j0)] = ring3.tile([P, 4, width], F32, name="gated")
-                nc.scalar.activation(out=gates[(g, j0)][:, t0 : t0 + per_bank, :], in_=bank[:], func=GELU)
+                    gates[(g, j0)] = ring3.tile([P, 4 // per_bank, width, per_bank], F32, name="gated")
+                nc.scalar.activation(
+                    out=gates[(g, j0)][:, t0 // per_bank], in_=bank[:].rearrange("p s c -> p c s"), func=GELU
+                )
 
         def gate_step(g, j0, width, step):
             for t0 in range(0, 4, BANK // width):
@@ -300,10 +308,12 @@ def tile_list_gelu_mix_biasP_kernel(
                         )
 
         def product(g, j0, c0):
+            gated = gates[(g, j0)]
+            per_bank = gated.shape[3]
             nc.vector.tensor_tensor(
-                as_words(h_words[g][:, 4 * (j0 + c0) : 4 * (j0 + c0 + P)]),
-                as_planes(up_banks[(g, j0 + c0)][:]),
-                as_planes(gates[(g, j0)][:, :, c0 : c0 + P]),
+                h_words[g][:, 4 * (j0 + c0) : 4 * (j0 + c0 + P)].rearrange("p (c b s) -> p c b s", c=P, s=per_bank),
+                up_banks[(g, j0 + c0)][:].rearrange("p (b s) c -> p c b s", s=per_bank),
+                gated[:, :, c0 : c0 + P, :].rearrange("p b c s -> p c b s"),
                 MULT,
             )
 

@@ -183,9 +183,12 @@ def tile_list_gelu_mix_biasP_kernel(
                         )
                 c0, c1 = 2 * P * u, 2 * P * (u + halves)
                 name = "first_w" if (a, g, u) == (0, 0, 1) else "wg_scales%d%d%d" % (a, g, u)
-                scales = kept(name, [P, c1 - c0], U8)
+                if (a, g, u) == (0, 0, 0):
+                    scales = x_scales[0][WD8_ROW:P, 0:UNIT]
+                else:
+                    scales = kept(name, [P, c1 - c0], U8)[:]
                 nc.vector.quantize_mx(
-                    out=codes[:, c0:c1].bitcast(FP8X4), scales=scales[:], in_=words[:, 4 * c0 : 4 * c1]
+                    out=codes[:, c0:c1].bitcast(FP8X4), scales=scales, in_=words[:, 4 * c0 : 4 * c1]
                 )
                 for t in range(2 * u, 2 * (u + halves)):
                     wg_scales[(a, g, t)] = scales[:, P * t - c0 : P * (t + 1) - c0]
@@ -254,7 +257,7 @@ def tile_list_gelu_mix_biasP_kernel(
         def pass_order(g, j0):
             return (0, 1) if g == 0 and j0 < 2 * UNIT else (1, 0)
 
-        def gate_pass(g, j0, width, step, t0):
+        def gate_pass(g, j0, width, step, t0, gelu=True):
             per_bank = BANK // width
             a = pass_order(g, j0)[step]
             places = slice(j0, j0 + width)
@@ -272,7 +275,13 @@ def tile_list_gelu_mix_biasP_kernel(
                     start=(step == 0 and s == 0),
                     stop=(step == 1 and s == per_bank - 1),
                 )
-            if step == 1:
+            if step == 1 and gelu:
+                gelu_bank(g, j0, width, t0)
+
+        def gelu_bank(g, j0, width, t0):
+            per_bank = BANK // width
+            bank = gate_banks[(g, j0, t0)]
+            if True:
                 if t0 == 0:
                     gates[(g, j0)] = ring3.tile([P, 4 // per_bank, width, per_bank], F32, name="gated")
                 nc.scalar.activation(
@@ -283,20 +292,20 @@ def tile_list_gelu_mix_biasP_kernel(
             for t0 in range(0, 4, BANK // width):
                 gate_pass(g, j0, width, step, t0)
 
-        def gate_unit(g, j0, width):
+        def gate_unit(g, j0, width, gelu=True):
             for t0 in range(0, 4, BANK // width):
                 for step in range(2):
-                    gate_pass(g, j0, width, step, t0)
+                    gate_pass(g, j0, width, step, t0, gelu)
 
         def up_passes(g, j0, width):
             passes = pass_order(g, j0)
             starts = range(j0, j0 + width, P)
             for j1 in starts:
                 up_banks[(g, j1)] = psum.tile([P, 4, P], F32, name="up_bank")
-            for a in passes:
-                for t in range(4):
-                    col0 = PASS * a + P * t
-                    for j1 in starts:
+            for j1 in starts:
+                for a in passes:
+                    for t in range(4):
+                        col0 = PASS * a + P * t
                         nc.tensor.matmul_mx(
                             out=up_banks[(g, j1)][:, t, :],
                             lhsT=wu_dealt[g][:, 2 * col0 : 2 * (col0 + P)].bitcast(FP4X4),
@@ -402,11 +411,19 @@ def tile_list_gelu_mix_biasP_kernel(
 
         for unit in units[:2]:
             hidden_unit(0, *unit)
-        quantise_wg(1, 1, [on_vector], False)
+        gate_unit(0, HALF, UNIT)
+        gate_unit(0, LAST, UNIT, False)
+        up_passes(0, HALF, UNIT)
+        up_passes(0, LAST, UNIT)
+        quantise_wg(1, 1, [on_vector], True)
         quantise_wg(0, 1, [on_scalar], True)
         deal_wu(1)
-        for unit in units[2:]:
-            hidden_unit(0, *unit)
+        for c0 in (0, P):
+            product(0, HALF, c0)
+        for t0 in (0, 2):
+            gelu_bank(0, LAST, UNIT, t0)
+        for c0 in (0, P):
+            product(0, LAST, c0)
         hidden_unit(1, 0, 256)
         quantise_h(1, 0, 256)
         deal_wd()

@@ -198,6 +198,8 @@ def tile_list_gelu_mix_biasP_kernel(
                 out=wu_dealt[g][:].bitcast(U16).rearrange("p (a t m) -> p a t m", a=2, t=4),
                 in_=wu_raw[g][:].bitcast(U16).rearrange("p a (m t) -> p a t m", t=4),
             )
+
+        def deal_wu_scales(g):
             nc.vector.tensor_copy(
                 out=wu_scale[g][:].rearrange("p (a t m) -> p a t m", a=2, t=4),
                 in_=wu_scale_raw[:, :, g * PASS : (g + 1) * PASS].rearrange("p a (m t) -> p a t m", t=4),
@@ -223,6 +225,8 @@ def tile_list_gelu_mix_biasP_kernel(
         spread_weights()
 
         deal_wu(0)
+        for g in range(2):
+            deal_wu_scales(g)
         gather(0, 0, HALF, HALF)
         gather(0, 0, 0, HALF)
         for i in (1, 2):
@@ -362,17 +366,15 @@ def tile_list_gelu_mix_biasP_kernel(
         def wd4_passes(bank, t0, j0, width, first):
             for s in range(2):
                 col0 = P * (t0 + s)
-                for c0 in range(0, width, P):
-                    part = slice(j0 + c0, j0 + c0 + P)
-                    nc.tensor.matmul_mx(
-                        out=bank[:, s, c0 : c0 + P],
-                        lhsT=wd4_dealt[:, 2 * col0 : 2 * (col0 + P)].bitcast(FP4X4),
-                        lhsT_scale=wd_scale[:, col0 : col0 + P],
-                        rhs=h_codes[1][:, part].bitcast(FP8X4),
-                        rhs_scale=h_scales[1][:, part],
-                        start=(first and s == 0 and c0 == 0),
-                        stop=(not first and s == 1 and c0 + P == width),
-                    )
+                nc.tensor.matmul_mx(
+                    out=bank[:, s, :],
+                    lhsT=wd4_dealt[:, 2 * col0 : 2 * (col0 + P)].bitcast(FP4X4),
+                    lhsT_scale=wd_scale[:, col0 : col0 + P],
+                    rhs=h_codes[1][:, j0 : j0 + width].bitcast(FP8X4),
+                    rhs_scale=h_scales[1][:, j0 : j0 + width],
+                    start=(first and s == 0),
+                    stop=(not first and s == 1),
+                )
 
         def output_bank(j0, width, t0, on_vector_engine=False, store=2):
             places = slice(j0, j0 + width)

@@ -9,6 +9,7 @@ FLOPS = 2 * J * (2 * K * R + R * N)
 F32 = mybir.dt.float32
 BF16 = mybir.dt.bfloat16
 I32 = mybir.dt.int32
+U32 = mybir.dt.uint32
 U16 = mybir.dt.uint16
 U8 = mybir.dt.uint8
 FP8X4 = mybir.dt.float8_e4m3fn_x4
@@ -194,7 +195,8 @@ def tile_list_gelu_mix_biasP_kernel(
                     wg_scales[(a, g, t)] = scales[:, P * t - c0 : P * (t + 1) - c0]
 
         def deal_wu(g):
-            nc.vector.tensor_copy(
+            copy = nc.scalar.copy if g else nc.vector.tensor_copy
+            copy(
                 out=wu_dealt[g][:].bitcast(U16).rearrange("p (a t m) -> p a t m", a=2, t=4),
                 in_=wu_raw[g][:].bitcast(U16).rearrange("p a (m t) -> p a t m", t=4),
             )
@@ -206,11 +208,11 @@ def tile_list_gelu_mix_biasP_kernel(
             )
 
         def deal_wd():
-            nc.vector.tensor_copy(
-                out=wd8_dealt[:].rearrange("p (u e m) -> p u m e", u=2, e=2),
-                in_=wd8_raw[:].rearrange("p (m u e) -> p u m e", u=2, e=2),
+            nc.scalar.copy(
+                out=wd8_dealt[:].bitcast(U32).rearrange("p (u e m) -> p u m e", u=2, e=2),
+                in_=wd8_raw[:].bitcast(U32).rearrange("p (m u e) -> p u m e", u=2, e=2),
             )
-            nc.vector.tensor_copy(
+            nc.scalar.copy(
                 out=wd4_dealt[:].bitcast(U16).rearrange("p (t m) -> p t m", t=4),
                 in_=wd4_raw[:].bitcast(U16).rearrange("p (m t) -> p t m", t=4),
             )

@@ -49,8 +49,6 @@ def tile_list_gelu_mix_biasP_kernel(
         def kept(name, shape, dtype):
             return keep.tile(shape, dtype, name=name, align_bytes=64)
 
-        offsets = keep.tile([P, J // 16], U16, name="offsets")
-
         wu_scale_raw = kept("wu_scale_raw", [P, 2, R], U8)
         wd_scale_raw = kept("wd_scale_raw", [P, N], U8)
         nc.vector.memset(wu_scale_raw[:].bitcast(I32), 0)
@@ -58,10 +56,13 @@ def tile_list_gelu_mix_biasP_kernel(
 
         first_w = kept("first_w", [P, UNIT], F32)
         weights = kept("weights", [P, J], F32)
-        x_planes = [[kept("x_plane%d%d" % (a, i), [P, T], F32) for i in range(4)] for a in range(2)]
+        x_planes = [
+            [keep.tile([P, T], F32, name="x_plane%d%d" % (a, i), align_bytes=256) for i in range(4)] for a in range(2)
+        ]
         wu_raw = [kept("wu_raw%d" % g, [P, 2, 2 * PASS], U8) for g in range(2)]
         wd8_raw = kept("wd8_raw", [P, N], I32)
         wd4_raw = kept("wd4_raw", [P, 2 * N], U8)
+        offsets = keep.tile([P, J // 16], U16, name="offsets")
         bias = kept("bias", [P, 4], F32)
         wg_raw = {}
 
@@ -70,7 +71,7 @@ def tile_list_gelu_mix_biasP_kernel(
             nc.sync.dma_start(out=x_planes[a][i][:], in_=rows[:, i, :])
 
         def load_wg(a, g):
-            raw = ring3.tile([P, 4, PASS], F32, name="f32_stage", bufs=4)
+            raw = ring3.tile([P, 4, PASS], F32, name="f32_stage", bufs=4, align_bytes=256)
             rows = wg[a * PASS : (a + 1) * PASS, g * PASS : (g + 1) * PASS]
             nc.sync.dma_start(out=raw[:], in_=rows.rearrange("(p i) r -> p i r", i=4))
             wg_raw[(a, g)] = raw
@@ -381,7 +382,7 @@ def tile_list_gelu_mix_biasP_kernel(
         def output_bank(j0, width, t0, on_vector_engine=False, store=2):
             places = slice(j0, j0 + width)
             if t0 == 0:
-                sums[j0] = ring3.tile([P, 4, width], F32, name="f32_stage", bufs=4)
+                sums[j0] = ring3.tile([P, 4, width], F32, name="f32_stage", bufs=4, align_bytes=256)
             y = sums[j0]
             order = (wd4_passes, wd8_passes) if width == UNIT else (wd8_passes, wd4_passes)
             bank = psum.tile([P, 2, width], F32, name="up_bank" if t0 else "gate_bank")

@@ -51,7 +51,9 @@ def tile_list_gelu_mix_biasP_kernel(
 
         wu_scale_raw = kept("wu_scale_raw", [P, 2, R], U8)
         wd_scale_raw = kept("wd_scale_raw", [P, N], U8)
-        nc.vector.memset(wu_scale_raw[:].bitcast(I32), 0)
+        nc.gpsimd.memset(wu_scale_raw[:].bitcast(I32), 0)
+        warm_up_zero = kept("warm_up_zero", [P, 1], F32)
+        nc.vector.memset(warm_up_zero[:], 0.0)
         nc.vector.memset(wd_scale_raw[:].bitcast(I32), 0)
 
         first_w = kept("first_w", [P, UNIT], F32)
@@ -64,17 +66,19 @@ def tile_list_gelu_mix_biasP_kernel(
         wd4_raw = kept("wd4_raw", [P, 2 * N], U8)
         offsets = keep.tile([P, J // 16], U16, name="offsets")
         bias = kept("bias", [P, 4], F32)
-        wg_raw = {}
+        wg_raw, wg_parts = {}, {}
 
         def load_plane(a, i):
             rows = xT[a * PASS : (a + 1) * PASS, :].rearrange("(p i) t -> p i t", i=4)
             nc.sync.dma_start(out=x_planes[a][i][:], in_=rows[:, i, :])
 
-        def load_wg(a, g):
-            raw = ring3.tile([P, 4, PASS], F32, name="f32_stage", bufs=4, align_bytes=256)
-            rows = wg[a * PASS : (a + 1) * PASS, g * PASS : (g + 1) * PASS]
-            nc.sync.dma_start(out=raw[:], in_=rows.rearrange("(p i) r -> p i r", i=4))
-            wg_raw[(a, g)] = raw
+        def load_wg(a, g, m0=0, m1=P):
+            if m0 == 0:
+                wg_raw[(a, g)] = ring3.tile([P, 4 * PASS], F32, name="f32_stage", bufs=4, align_bytes=256)
+            rows = wg[a * PASS : (a + 1) * PASS, g * PASS + 4 * m0 : g * PASS + 4 * m1]
+            raw = wg_raw[(a, g)][:, 16 * m0 : 16 * m1].rearrange("p (i r) -> p i r", i=4)
+            nc.sync.dma_start(out=raw, in_=rows.rearrange("(p i) r -> p i r", i=4))
+            wg_parts[(a, g, m0)] = raw
 
         def load_wu(g):
             cols = wu_words[:, :, 2 * g * PASS : 2 * (g + 1) * PASS]
@@ -83,18 +87,19 @@ def tile_list_gelu_mix_biasP_kernel(
         def place_w(j0, j1):
             return first_w[:, j0:j1] if j1 <= UNIT else weights[:, j0:j1]
 
-        def spread_weights():
+        def spread_weights(h, copy):
             turned = psum.tile([P, P], F32, name="up_bank")
-            nc.tensor.transpose(turned[:], w_rows[:], identity[:])
+            nc.tensor.transpose(turned[:], w_rows[h][:], identity[:])
             by_block = turned[:].rearrange("k (r jb) -> k jb r", jb=4)
-            nc.scalar.copy(out=w_spread[:], in_=by_block.unsqueeze(3).to_broadcast([P, 4, 32, 4]))
+            nc.scalar.copy(out=w_spread[h][:], in_=by_block.unsqueeze(3).to_broadcast([P, 4, 32, 4]))
             bank = psum.tile([P, HALF], F32, name="gate_bank")
             for jb in range(4):
                 nc.tensor.transpose(
-                    bank[:, jb * P : (jb + 1) * P], w_spread[:, jb].rearrange("k r d -> k (r d)"), identity[:]
+                    bank[:, jb * P : (jb + 1) * P], w_spread[h][:, jb].rearrange("k r d -> k (r d)"), identity[:]
                 )
-            nc.scalar.copy(out=weights[:, 0:HALF], in_=bank[:])
-            nc.scalar.copy(out=first_w[:], in_=bank[:, 0:UNIT])
+            copy(out=weights[:, h * HALF : (h + 1) * HALF], in_=bank[:])
+            if h == 0:
+                nc.scalar.copy(out=first_w[:], in_=bank[:, 0:UNIT])
 
         def load_wu_scales():
             for row in range(4):
@@ -113,13 +118,14 @@ def tile_list_gelu_mix_biasP_kernel(
                         out=wd_scale_raw[row0 + row : P : 32, :].bitcast(I32), in_=scales[0, row:16:4, :].bitcast(I32)
                     )
 
-        w_rows = kept("wg_codes00", [P, P], F32)
-        w_spread = kept("wg_codes10", [P, 4, 32, 4], F32)
+        w_rows = [kept(name, [P, P], F32) for name in ("wg_codes00", "wg_codes11")]
+        w_spread = [kept(name, [P, 4, 32, 4], F32) for name in ("wg_codes10", "wd8_dealt")]
         identity = kept("wg_codes01", [P, P], F32)
         make_identity(nc, identity[:])
-        nc.sync.dma_start(out=w_rows[:], in_=wgt[0:P:4, 0:HALF].rearrange("r (jb k) -> r jb k", k=P))
+        for h in range(2):
+            rows = wgt[0:P:4, h * HALF : (h + 1) * HALF]
+            nc.sync.dma_start(out=w_rows[h][:], in_=rows.rearrange("r (jb k) -> r jb k", k=P))
         load_wu(0)
-        nc.sync.dma_start(out=weights[:, HALF:J], in_=wgt[:, HALF:J])
         load_wu_scales()
         load_plane(0, 0)
         nc.sync.dma_start(offsets[:], offs)
@@ -166,37 +172,35 @@ def tile_list_gelu_mix_biasP_kernel(
                 in_=x_words[a][:, 4 * j0 : 4 * (j0 + width)],
             )
 
-        def quantise_wg(a, g, copies, split):
-            words = ring2.tile([P, 4 * PASS], BF16, name="wg_words", align_bytes=64)
-            dealt = words[:].rearrange("p (u e m i) -> p u m i e", u=2, e=2, i=4)
-            raw = wg_raw[(a, g)][:].rearrange("p i (m u e) -> p u m i e", u=2, e=2)
-            codes = wg_codes[(a, g)] = kept("wg_codes%d%d" % (a, g), [P, PASS], I32)
-            halves = 1 if split else 2
-            for u in range(0, 2, halves):
-                step = P // len(copies)
-                for m0 in range(0, P, step):
-                    copy = copies[m0 // step]
-                    if split:
-                        copy(out=dealt[:, u, m0 : m0 + step], in_=raw[:, u, m0 : m0 + step])
-                    else:
-                        copy(
-                            out=words[:].rearrange("p (t m i) -> p m i t", t=4, i=4),
-                            in_=wg_raw[(a, g)][:].rearrange("p i (m t) -> p m i t", t=4),
-                        )
-                c0, c1 = 2 * P * u, 2 * P * (u + halves)
-                name = "first_w" if (a, g, u) == (0, 0, 1) else "wg_scales%d%d%d" % (a, g, u)
-                if (a, g, u) == (0, 0, 0):
-                    scales = x_scales[0][WD8_ROW:P, 0:UNIT]
-                else:
-                    scales = kept(name, [P, c1 - c0], U8)[:]
-                nc.vector.quantize_mx(
-                    out=codes[:, c0:c1].bitcast(FP8X4), scales=scales, in_=words[:, 4 * c0 : 4 * c1]
-                )
-                for t in range(2 * u, 2 * (u + halves)):
-                    wg_scales[(a, g, t)] = scales[:, P * t - c0 : P * (t + 1) - c0]
+        wg_words = {}
 
-        def deal_wu(g):
-            copy = nc.scalar.copy if g else nc.vector.tensor_copy
+        def round_wg(copy, a, g, u, m0=0, m1=P):
+            if (a, g) not in wg_words:
+                wg_words[(a, g)] = ring2.tile([P, 4 * PASS], BF16, name="wg_words", align_bytes=64)
+                wg_codes[(a, g)] = kept("wg_codes%d%d" % (a, g), [P, PASS], I32)
+            dealt = wg_words[(a, g)][:].rearrange("p (u e m i) -> p u m i e", u=2, e=2, i=4)
+            raw = wg_parts[(a, g, m0)].rearrange("p i (m u e) -> p u m i e", u=2, e=2)
+            copy(out=dealt[:, u, m0:m1], in_=raw[:, u])
+
+        def quantise_wg(a, g, u):
+            c0, c1 = 2 * P * u, 2 * P * (u + 1)
+            name = "first_w" if (a, g, u) == (0, 0, 1) else "wg_scales%d%d%d" % (a, g, u)
+            if (a, g, u) == (0, 0, 0):
+                scales = x_scales[0][WD8_ROW:P, 0:UNIT]
+            else:
+                scales = kept(name, [P, c1 - c0], U8)[:]
+            nc.vector.quantize_mx(
+                out=wg_codes[(a, g)][:, c0:c1].bitcast(FP8X4), scales=scales, in_=wg_words[(a, g)][:, 4 * c0 : 4 * c1]
+            )
+            for t in (2 * u, 2 * u + 1):
+                wg_scales[(a, g, t)] = scales[:, P * t - c0 : P * (t + 1) - c0]
+
+        def prepare_wg(copy, a, g):
+            for u in range(2):
+                round_wg(copy, a, g, u)
+                quantise_wg(a, g, u)
+
+        def deal_wu(copy, g):
             copy(
                 out=wu_dealt[g][:].bitcast(U16).rearrange("p (a t m) -> p a t m", a=2, t=4),
                 in_=wu_raw[g][:].bitcast(U16).rearrange("p a (m t) -> p a t m", t=4),
@@ -224,14 +228,15 @@ def tile_list_gelu_mix_biasP_kernel(
 
         on_scalar, on_vector = nc.scalar.copy, nc.vector.tensor_copy
         table_warm_up = kept("table_warm_up", [P, 1], F32)
-        nc.scalar.activation(out=table_warm_up[:], in_=identity[:, 0:1], func=GELU)
-        spread_weights()
+        nc.scalar.activation(out=table_warm_up[:], in_=warm_up_zero[:], func=GELU)
 
-        deal_wu(0)
+        deal_wu(on_vector, 0)
         for g in range(2):
             deal_wu_scales(g)
-        gather(0, 0, HALF, HALF)
+        spread_weights(0, on_vector)
+        spread_weights(1, on_scalar)
         gather(0, 0, 0, HALF)
+        gather(0, 0, HALF, HALF)
         for i in (1, 2):
             gather(0, i, 0, J)
         for j0 in (0, HALF):
@@ -248,9 +253,9 @@ def tile_list_gelu_mix_biasP_kernel(
             round_x(on_scalar, 1, 0, 4, j0, width)
             quantise_x(1, j0, width)
             if j0 == 0:
-                quantise_wg(0, 0, [on_scalar], True)
+                prepare_wg(on_scalar, 0, 0)
             if j0 == UNIT:
-                quantise_wg(1, 0, [on_vector], True)
+                prepare_wg(on_vector, 1, 0)
 
         h_codes = [kept("h_codes%d" % g, [P, J], I32) for g in range(2)]
         h_scales = [kept("h_scales%d" % g, [P, J], U8) for g in range(2)]
@@ -379,8 +384,7 @@ def tile_list_gelu_mix_biasP_kernel(
                     stop=(not first and s == 1),
                 )
 
-        def output_bank(j0, width, t0, on_vector_engine=False, store=2):
-            places = slice(j0, j0 + width)
+        def output_bank(j0, width, t0, on_vector_engine=False):
             if t0 == 0:
                 sums[j0] = ring3.tile([P, 4, width], F32, name="f32_stage", bufs=4, align_bytes=256)
             y = sums[j0]
@@ -396,20 +400,25 @@ def tile_list_gelu_mix_biasP_kernel(
                     nc.scalar.activation(
                         out=y[:, t, :], in_=bank[:, t - t0, :], func=IDENTITY, bias=bias[:, t : t + 1], scale=1.0
                     )
-            if store:
-                rows = slice(t0 + 2 - store, t0 + 2)
-                nc.sync.dma_start(out=y_rows[:, rows, places], in_=y[:, rows, :])
 
         def output_sums(j0, width, vector_banks=()):
-            output_bank(j0, width, 0, 0 in vector_banks, 0)
-            output_bank(j0, width, 2, 2 in vector_banks, 4)
+            output_bank(j0, width, 0, 0 in vector_banks)
+            output_bank(j0, width, 2, 2 in vector_banks)
+            nc.sync.dma_start(out=y_rows[:, :, j0 : j0 + width], in_=sums[j0][:])
 
-        def output_codes(j0, width, copy, stored):
+        y_words = {}
+
+        def round_y(j0, width, copy):
+            y_words[j0] = ring2.tile([P, 4 * width], BF16, name="y_words", align_bytes=64)
+            copy(out=as_words(y_words[j0][:]), in_=as_planes(sums[j0][:]))
+
+        def quantise_y(j0, width, stored):
             places = slice(j0, j0 + width)
-            y = sums[j0]
-            y_words = ring2.tile([P, 4 * width], BF16, name="y_words", align_bytes=64)
-            copy(out=as_words(y_words[:]), in_=as_planes(y[:]))
-            nc.vector.quantize_mx(out=y_codes[:, places].bitcast(FP8X4), scales=y_scales[:, places], in_=y_words[:])
+            nc.vector.quantize_mx(
+                out=y_codes[:, places].bitcast(FP8X4),
+                scales=y_scales[:, places],
+                in_=y_words[j0][:],
+            )
             if stored:
                 done = slice(j0 + width - stored, j0 + width)
                 nc.sync.dma_start(out=y_word_rows[:, done], in_=y_codes[:, done])
@@ -420,9 +429,9 @@ def tile_list_gelu_mix_biasP_kernel(
         gate_unit(0, LAST, UNIT, False)
         up_passes(0, HALF, UNIT)
         up_passes(0, LAST, UNIT)
-        quantise_wg(1, 1, [on_vector], True)
-        quantise_wg(0, 1, [on_scalar], True)
-        deal_wu(1)
+        prepare_wg(on_vector, 1, 1)
+        prepare_wg(on_scalar, 0, 1)
+        deal_wu(on_scalar, 1)
         for c0 in (0, P):
             product(0, HALF, c0)
         for t0 in (0, 2):
@@ -439,24 +448,30 @@ def tile_list_gelu_mix_biasP_kernel(
         output_sums(0, 256, ())
         up_unit(1, 512, 256)
         quantise_h(1, 512, 256)
-        output_codes(0, 256, on_vector, 256)
+        round_y(0, 256, on_vector)
+        quantise_y(0, 256, 256)
         quantise_h(0, 512, 512)
         gate_unit(1, 768, 128)
         output_sums(256, 256, ())
         up_unit(1, 768, 128)
         quantise_h(1, 768, 128)
-        output_codes(256, 256, on_vector, 256)
+        round_y(256, 256, on_vector)
+        quantise_y(256, 256, 256)
         gate_unit(1, 896, 128)
         output_sums(512, 128, ())
         up_unit(1, 896, 128)
         quantise_h(1, 896, 128)
-        output_codes(512, 128, on_vector, 0)
+        round_y(512, 128, on_vector)
+        quantise_y(512, 128, 0)
         output_sums(640, 128, ())
         output_sums(768, 128, ())
-        output_codes(640, 128, on_vector, 256)
+        round_y(640, 128, on_vector)
+        quantise_y(640, 128, 256)
         output_sums(896, 128, (2,))
-        output_codes(768, 128, on_vector, 0)
-        output_codes(896, 128, on_vector, 256)
+        round_y(768, 128, on_vector)
+        quantise_y(768, 128, 0)
+        round_y(896, 128, on_vector)
+        quantise_y(896, 128, 256)
 
         for row in range(4):
             queue = nc.sync if row % 2 else nc.scalar

@@ -174,13 +174,23 @@ def tile_list_gelu_mix_biasP_kernel(
 
         wg_words = {}
 
+        def half_words(a, g, u):
+            if (a, g, u) == (0, 1, 0):
+                return wg_words[(1, 1)][:, 0 : 8 * P]
+            if (a, g, u) == (1, 1, 1):
+                return gates[(0, UNIT)][:].rearrange("p b c s -> p (b c s)")[:, 0:PASS].bitcast(BF16)
+            return wg_words[(a, g)][:, 8 * P * u : 8 * P * (u + 1)]
+
         def round_wg(copy, a, g, u, m0=0, m1=P):
             if (a, g) not in wg_words:
                 wg_words[(a, g)] = ring2.tile([P, 4 * PASS], BF16, name="wg_words", align_bytes=64)
                 wg_codes[(a, g)] = kept("wg_codes%d%d" % (a, g), [P, PASS], I32)
-            dealt = wg_words[(a, g)][:].rearrange("p (u e m i) -> p u m i e", u=2, e=2, i=4)
+            dealt = half_words(a, g, u).rearrange("p (e m i) -> p m i e", e=2, i=4)
             raw = wg_parts[(a, g, m0)].rearrange("p i (m u e) -> p u m i e", u=2, e=2)
-            copy(out=dealt[:, u, m0:m1], in_=raw[:, u])
+            if copy is on_gpsimd:
+                copy(out=dealt.rearrange("p m i e -> p e m i"), in_=raw[:, u].rearrange("p m i e -> p e m i"))
+            else:
+                copy(out=dealt[:, m0:m1], in_=raw[:, u])
 
         def quantise_wg(a, g, u):
             c0, c1 = 2 * P * u, 2 * P * (u + 1)
@@ -190,7 +200,7 @@ def tile_list_gelu_mix_biasP_kernel(
             else:
                 scales = kept(name, [P, c1 - c0], U8)[:]
             nc.vector.quantize_mx(
-                out=wg_codes[(a, g)][:, c0:c1].bitcast(FP8X4), scales=scales, in_=wg_words[(a, g)][:, 4 * c0 : 4 * c1]
+                out=wg_codes[(a, g)][:, c0:c1].bitcast(FP8X4), scales=scales, in_=half_words(a, g, u)
             )
             for t in (2 * u, 2 * u + 1):
                 wg_scales[(a, g, t)] = scales[:, P * t - c0 : P * (t + 1) - c0]
@@ -227,6 +237,10 @@ def tile_list_gelu_mix_biasP_kernel(
             )
 
         on_scalar, on_vector = nc.scalar.copy, nc.vector.tensor_copy
+
+        def on_gpsimd(out, in_):
+            nc.gpsimd.tensor_scalar(out=out, in0=in_, scalar1=1.0, scalar2=0.0, op0=MULT, op1=ADD)
+
         table_warm_up = kept("table_warm_up", [P, 1], F32)
         nc.scalar.activation(out=table_warm_up[:], in_=warm_up_zero[:], func=GELU)
 
@@ -430,7 +444,10 @@ def tile_list_gelu_mix_biasP_kernel(
         up_passes(0, HALF, UNIT)
         up_passes(0, LAST, UNIT)
         prepare_wg(on_vector, 1, 1)
-        prepare_wg(on_scalar, 0, 1)
+        round_wg(on_gpsimd, 0, 1, 0)
+        round_wg(on_scalar, 0, 1, 1)
+        quantise_wg(0, 1, 0)
+        quantise_wg(0, 1, 1)
         deal_wu(on_scalar, 1)
         for c0 in (0, P):
             product(0, HALF, c0)

from contextlib import ExitStack

import concourse.mybir as mybir
from concourse.masks import make_identity

K, R, N, T, J = 1024, 1024, 512, 2048, 1024
FLOPS = 2 * J * (2 * K * R + R * N)

F32 = mybir.dt.float32
BF16 = mybir.dt.bfloat16
I32 = mybir.dt.int32
U32 = mybir.dt.uint32
U16 = mybir.dt.uint16
U8 = mybir.dt.uint8
FP8X4 = mybir.dt.float8_e4m3fn_x4
FP4X4 = mybir.dt.float4_e2m1fn_x4
MULT = mybir.AluOpType.mult
ADD = mybir.AluOpType.add
GELU = mybir.ActivationFunctionType.Gelu_apprx_tanh
IDENTITY = mybir.ActivationFunctionType.Identity

P = 128
PASS = 512
BANK = 512
HALF = J // 2
UNIT = 256
LAST = J - UNIT
WD8_ROW = 4


def as_words(words):
    return words.rearrange("p (c e t) -> p c t e", e=4, t=4)


def as_planes(planes):
    return planes.rearrange("p t (c e) -> p c t e", e=4)


def tile_list_gelu_mix_biasP_kernel(
    tc, xT, wgt, wg, wu_words, wu_scales, wd8_words, wd8_scales, wd4_words, wd4_scales, b, offs, out_0, out_1, out_2
):
    nc = tc.nc
    with ExitStack() as ctx:
        keep = ctx.enter_context(tc.tile_pool(name="keep", bufs=1))
        ring2 = ctx.enter_context(tc.tile_pool(name="ring2", bufs=2))
        ring3 = ctx.enter_context(tc.tile_pool(name="ring3", bufs=3))
        psum = ctx.enter_context(tc.psum_pool(name="psum", bufs=4))

        def kept(name, shape, dtype):
            return keep.tile(shape, dtype, name=name, align_bytes=64)

        wu_scale_raw = kept("wu_scale_raw", [P, 2, R], U8)
        wd_scale_raw = kept("wd_scale_raw", [P, N], U8)
        nc.gpsimd.memset(wu_scale_raw[:].bitcast(I32), 0)
        warm_up_zero = kept("warm_up_zero", [P, 1], F32)
        nc.vector.memset(warm_up_zero[:], 0.0)
        nc.vector.memset(wd_scale_raw[:].bitcast(I32), 0)

        first_w = kept("first_w", [P, UNIT], F32)
        weights = kept("weights", [P, J], F32)
        x_planes = [
            [keep.tile([P, T], F32, name="x_plane%d%d" % (a, i), align_bytes=256) for i in range(4)] for a in range(2)
        ]
        wu_raw = [kept("wu_raw%d" % g, [P, 2, 2 * PASS], U8) for g in range(2)]
        wd8_raw = kept("wd8_raw", [P, N], I32)
        wd4_raw = kept("wd4_raw", [P, 2 * N], U8)
        offsets = keep.tile([P, J // 16], U16, name="offsets")
        bias = kept("bias", [P, 4], F32)
        wg_raw, wg_parts = {}, {}

        def load_plane(a, i):
            rows = xT[a * PASS : (a + 1) * PASS, :].rearrange("(p i) t -> p i t", i=4)
            nc.sync.dma_start(out=x_planes[a][i][:], in_=rows[:, i, :])

        def load_wg(a, g, m0=0, m1=P):
            if m0 == 0:
                wg_raw[(a, g)] = ring3.tile([P, 4 * PASS], F32, name="f32_stage", bufs=4, align_bytes=256)
            rows = wg[a * PASS : (a + 1) * PASS, g * PASS + 4 * m0 : g * PASS + 4 * m1]
            raw = wg_raw[(a, g)][:, 16 * m0 : 16 * m1].rearrange("p (i r) -> p i r", i=4)
            nc.sync.dma_start(out=raw, in_=rows.rearrange("(p i) r -> p i r", i=4))
            wg_parts[(a, g, m0)] = raw

        def load_wu(g):
            cols = wu_words[:, :, 2 * g * PASS : 2 * (g + 1) * PASS]
            nc.sync.dma_start(out=wu_raw[g][:].bitcast(I32), in_=cols.rearrange("a p c -> p a c").bitcast(I32))

        def place_w(j0, j1):
            return first_w[:, j0:j1] if j1 <= UNIT else weights[:, j0:j1]

        def spread_weights(h, copy):
            turned = psum.tile([P, P], F32, name="up_bank")
            nc.tensor.transpose(turned[:], w_rows[h][:], identity[:])
            by_block = turned[:].rearrange("k (r jb) -> k jb r", jb=4)
            nc.scalar.copy(out=w_spread[h][:], in_=by_block.unsqueeze(3).to_broadcast([P, 4, 32, 4]))
            bank = psum.tile([P, HALF], F32, name="gate_bank")
            for jb in range(4):
                nc.tensor.transpose(
                    bank[:, jb * P : (jb + 1) * P], w_spread[h][:, jb].rearrange("k r d -> k (r d)"), identity[:]
                )
            copy(out=weights[:, h * HALF : (h + 1) * HALF], in_=bank[:])
            if h == 0:
                nc.scalar.copy(out=first_w[:], in_=bank[:, 0:UNIT])

        def load_wu_scales():
            for row in range(4):
                nc.sync.dma_start(
                    out=wu_scale_raw[row:P:32, :, :].bitcast(I32),
                    in_=wu_scales[:, row:16:4, :].rearrange("a q r -> q a r").bitcast(I32),
                )

        def load_wd():
            nc.sync.dma_start(out=wd8_raw[:], in_=wd8_words[0].rearrange("p n i -> p (n i)").bitcast(I32))
            nc.sync.dma_start(out=wd4_raw[:].bitcast(I32), in_=wd4_words[0].bitcast(I32))
            nc.sync.dma_start(out=bias[:], in_=b.rearrange("(p t) -> p t", t=4))
            for row0, scales in ((WD8_ROW, wd8_scales), (0, wd4_scales)):
                for row in range(4):
                    nc.sync.dma_start(
                        out=wd_scale_raw[row0 + row : P : 32, :].bitcast(I32), in_=scales[0, row:16:4, :].bitcast(I32)
                    )

        w_rows = [kept(name, [P, P], F32) for name in ("wg_codes00", "wg_codes11")]
        w_spread = [kept(name, [P, 4, 32, 4], F32) for name in ("wg_codes10", "wd8_dealt")]
        identity = kept("wg_codes01", [P, P], F32)
        make_identity(nc, identity[:])
        for h in range(2):
            rows = wgt[0:P:4, h * HALF : (h + 1) * HALF]
            nc.sync.dma_start(out=w_rows[h][:], in_=rows.rearrange("r (jb k) -> r jb k", k=P))
        load_wu(0)
        load_wu_scales()
        load_plane(0, 0)
        nc.sync.dma_start(offsets[:], offs)
        for i in range(1, 4):
            load_plane(0, i)
        for i in range(3):
            load_plane(1, i)
        load_wg(0, 0)
        load_plane(1, 3)
        load_wg(1, 0)
        load_wg(1, 1)
        load_wg(0, 1)
        load_wu(1)
        load_wd()

        x_codes = [kept("x_codes%d" % a, [P, J], I32) for a in range(2)]
        x_scales = [kept("x_scales%d" % a, [P, J], U8) for a in range(2)]
        wg_codes, wg_scales = {}, {}
        wu_dealt = [kept("wu_dealt%d" % g, [P, 2 * 2 * PASS], U8) for g in range(2)]
        wu_scale = [kept("wu_scale%d" % g, [P, 2 * PASS], U8) for g in range(2)]
        wd8_dealt = kept("wd8_dealt", [P, N], I32)
        wd4_dealt = kept("wd4_dealt", [P, 2 * N], U8)
        wd_scale = kept("wd_scale", [P, N], U8)
        picked = [kept("picked%d" % a, [P, 4, J], F32) for a in range(2)]
        x_words = [kept("x_words%d" % a, [P, 4 * J], BF16) for a in range(2)]

        def gather(a, i, j0, width):
            nc.vector.tensor_tensor(
                picked[a][:, i, j0 : j0 + width],
                x_planes[a][i][:].indirect(offsets[:, j0 // 16 : (j0 + width) // 16]),
                place_w(j0, j0 + width),
                MULT,
            )

        def round_x(copy, a, i0, planes, j0, width):
            words = as_words(x_words[a][:, 4 * j0 : 4 * (j0 + width)])
            copy(out=words[:, :, i0 : i0 + planes, :], in_=as_planes(picked[a][:, i0 : i0 + planes, j0 : j0 + width]))

        def quantise_x(a, j0, width):
            places = slice(j0, j0 + width)
            nc.vector.quantize_mx(
                out=x_codes[a][:, places].bitcast(FP8X4),
                scales=x_scales[a][:, places],
                in_=x_words[a][:, 4 * j0 : 4 * (j0 + width)],
            )

        wg_words = {}

        def half_words(a, g, u):
            if (a, g, u) == (0, 1, 0):
                return wg_words[(1, 1)][:, 0 : 8 * P]
            if (a, g, u) == (1, 1, 1):
                return gates[(0, UNIT)][:].rearrange("p b c s -> p (b c s)")[:, 0:PASS].bitcast(BF16)
            return wg_words[(a, g)][:, 8 * P * u : 8 * P * (u + 1)]

        def round_wg(copy, a, g, u, m0=0, m1=P):
            if (a, g) not in wg_words:
                wg_words[(a, g)] = ring2.tile([P, 4 * PASS], BF16, name="wg_words", align_bytes=64)
                wg_codes[(a, g)] = kept("wg_codes%d%d" % (a, g), [P, PASS], I32)
            dealt = half_words(a, g, u).rearrange("p (e m i) -> p m i e", e=2, i=4)
            raw = wg_parts[(a, g, m0)].rearrange("p i (m u e) -> p u m i e", u=2, e=2)
            if copy is on_gpsimd:
                copy(out=dealt.rearrange("p m i e -> p e m i"), in_=raw[:, u].rearrange("p m i e -> p e m i"))
            else:
                copy(out=dealt[:, m0:m1], in_=raw[:, u])

        def quantise_wg(a, g, u):
            c0, c1 = 2 * P * u, 2 * P * (u + 1)
            name = "first_w" if (a, g, u) == (0, 0, 1) else "wg_scales%d%d%d" % (a, g, u)
            if (a, g, u) == (0, 0, 0):
                scales = x_scales[0][WD8_ROW:P, 0:UNIT]
            else:
                scales = kept(name, [P, c1 - c0], U8)[:]
            nc.vector.quantize_mx(
                out=wg_codes[(a, g)][:, c0:c1].bitcast(FP8X4), scales=scales, in_=half_words(a, g, u)
            )
            for t in (2 * u, 2 * u + 1):
                wg_scales[(a, g, t)] = scales[:, P * t - c0 : P * (t + 1) - c0]

        def prepare_wg(copy, a, g):
            for u in range(2):
                round_wg(copy, a, g, u)
                quantise_wg(a, g, u)

        def deal_wu(copy, g):
            copy(
                out=wu_dealt[g][:].bitcast(U16).rearrange("p (a t m) -> p a t m", a=2, t=4),
                in_=wu_raw[g][:].bitcast(U16).rearrange("p a (m t) -> p a t m", t=4),
            )

        def deal_wu_scales(g):
            nc.vector.tensor_copy(
                out=wu_scale[g][:].rearrange("p (a t m) -> p a t m", a=2, t=4),
                in_=wu_scale_raw[:, :, g * PASS : (g + 1) * PASS].rearrange("p a (m t) -> p a t m", t=4),
            )

        def deal_wd():
            nc.scalar.copy(
                out=wd8_dealt[:].bitcast(U32).rearrange("p (u e m) -> p u m e", u=2, e=2),
                in_=wd8_raw[:].bitcast(U32).rearrange("p (m u e) -> p u m e", u=2, e=2),
            )
            nc.scalar.copy(
                out=wd4_dealt[:].bitcast(U16).rearrange("p (t m) -> p t m", t=4),
                in_=wd4_raw[:].bitcast(U16).rearrange("p (m t) -> p t m", t=4),
            )
            nc.vector.tensor_copy(
                out=wd_scale[:].rearrange("p (t m) -> p t m", t=4),
                in_=wd_scale_raw[:].rearrange("p (m t) -> p t m", t=4),
            )

        on_scalar, on_vector = nc.scalar.copy, nc.vector.tensor_copy

        def on_gpsimd(out, in_):
            nc.gpsimd.tensor_scalar(out=out, in0=in_, scalar1=1.0, scalar2=0.0, op0=MULT, op1=ADD)

        table_warm_up = kept("table_warm_up", [P, 1], F32)
        nc.scalar.activation(out=table_warm_up[:], in_=warm_up_zero[:], func=GELU)

        deal_wu(on_vector, 0)
        for g in range(2):
            deal_wu_scales(g)
        spread_weights(0, on_vector)
        spread_weights(1, on_scalar)
        gather(0, 0, 0, HALF)
        gather(0, 0, HALF, HALF)
        for i in (1, 2):
            gather(0, i, 0, J)
        for j0 in (0, HALF):
            gather(0, 3, j0, HALF)
        for j0 in range(0, J, HALF):
            round_x(on_scalar, 0, 0, 4, j0, HALF)
            quantise_x(0, j0, HALF)
        for i in range(3):
            gather(1, i, 0, J)
        units = [(j0, UNIT) for j0 in range(0, J, UNIT)]
        for j0, width in units:
            if j0 < LAST:
                gather(1, 3, j0, width if j0 < HALF else HALF)
            round_x(on_scalar, 1, 0, 4, j0, width)
            quantise_x(1, j0, width)
            if j0 == 0:
                prepare_wg(on_scalar, 0, 0)
            if j0 == UNIT:
                prepare_wg(on_vector, 1, 0)

        h_codes = [kept("h_codes%d" % g, [P, J], I32) for g in range(2)]
        h_scales = [kept("h_scales%d" % g, [P, J], U8) for g in range(2)]
        h_words = [kept(name, [P, 4 * J], BF16) for name in ("h_words0", "x_words0")]
        gates, sums = {}, {}
        y_codes = kept("y_codes", [P, J], I32)
        y_scales = kept("y_scales", [P, J], U8)

        gate_banks, up_banks = {}, {}

        def pass_order(g, j0):
            return (0, 1) if g == 0 and j0 < 2 * UNIT else (1, 0)

        def gate_pass(g, j0, width, step, t0, gelu=True):
            per_bank = BANK // width
            a = pass_order(g, j0)[step]
            places = slice(j0, j0 + width)
            if step == 0:
                gate_banks[(g, j0, t0)] = psum.tile([P, per_bank, width], F32, name="gate_bank")
            bank = gate_banks[(g, j0, t0)]
            for s in range(per_bank):
                cols = slice(P * (t0 + s), P * (t0 + s + 1))
                nc.tensor.matmul_mx(
                    out=bank[:, s, :],
                    lhsT=wg_codes[(a, g)][:, cols].bitcast(FP8X4),
                    lhsT_scale=wg_scales[(a, g, t0 + s)],
                    rhs=x_codes[a][:, places].bitcast(FP8X4),
                    rhs_scale=x_scales[a][:, places],
                    start=(step == 0 and s == 0),
                    stop=(step == 1 and s == per_bank - 1),
                )
            if step == 1 and gelu:
                gelu_bank(g, j0, width, t0)

        def gelu_bank(g, j0, width, t0):
            per_bank = BANK // width
            bank = gate_banks[(g, j0, t0)]
            if True:
                if t0 == 0:
                    gates[(g, j0)] = ring3.tile([P, 4 // per_bank, width, per_bank], F32, name="gated")
                nc.scalar.activation(
                    out=gates[(g, j0)][:, t0 // per_bank], in_=bank[:].rearrange("p s c -> p c s"), func=GELU
                )

        def gate_step(g, j0, width, step):
            for t0 in range(0, 4, BANK // width):
                gate_pass(g, j0, width, step, t0)

        def gate_unit(g, j0, width, gelu=True):
            for t0 in range(0, 4, BANK // width):
                for step in range(2):
                    gate_pass(g, j0, width, step, t0, gelu)

        def up_passes(g, j0, width):
            passes = pass_order(g, j0)
            starts = range(j0, j0 + width, P)
            for j1 in starts:
                up_banks[(g, j1)] = psum.tile([P, 4, P], F32, name="up_bank")
            for j1 in starts:
                for a in passes:
                    for t in range(4):
                        col0 = PASS * a + P * t
                        nc.tensor.matmul_mx(
                            out=up_banks[(g, j1)][:, t, :],
                            lhsT=wu_dealt[g][:, 2 * col0 : 2 * (col0 + P)].bitcast(FP4X4),
                            lhsT_scale=wu_scale[g][:, col0 : col0 + P],
                            rhs=x_codes[a][:, j1 : j1 + P].bitcast(FP8X4),
                            rhs_scale=x_scales[a][:, j1 : j1 + P],
                            start=(a == passes[0] and t == 0),
                            stop=(a == passes[1] and t == 3),
                        )

        def product(g, j0, c0):
            gated = gates[(g, j0)]
            per_bank = gated.shape[3]
            nc.vector.tensor_tensor(
                h_words[g][:, 4 * (j0 + c0) : 4 * (j0 + c0 + P)].rearrange("p (c b s) -> p c b s", c=P, s=per_bank),
                up_banks[(g, j0 + c0)][:].rearrange("p (b s) c -> p c b s", s=per_bank),
                gated[:, :, c0 : c0 + P, :].rearrange("p b c s -> p c b s"),
                MULT,
            )

        def up_unit(g, j0, width):
            up_passes(g, j0, width)
            for c0 in range(0, width, P):
                product(g, j0, c0)

        def hidden_unit(g, j0, width):
            gate_unit(g, j0, width)
            up_unit(g, j0, width)

        def quantise_h(g, j0, width):
            places = slice(j0, j0 + width)
            nc.vector.quantize_mx(
                out=h_codes[g][:, places].bitcast(FP8X4),
                scales=h_scales[g][:, places],
                in_=h_words[g][:, 4 * j0 : 4 * (j0 + width)],
            )

        y_rows = out_0.rearrange("(p t) j -> p t j", t=4)
        y_word_rows = out_1[0].rearrange("p j i -> p (j i)").bitcast(I32)

        def wd8_passes(bank, t0, j0, width, first):
            for s in range(2):
                cols = slice(P * (t0 + s), P * (t0 + s + 1))
                nc.tensor.matmul_mx(
                    out=bank[:, s, :],
                    lhsT=wd8_dealt[:, cols].bitcast(FP8X4),
                    lhsT_scale=wd_scale[WD8_ROW:P, cols],
                    rhs=h_codes[0][:, j0 : j0 + width].bitcast(FP8X4),
                    rhs_scale=h_scales[0][:, j0 : j0 + width],
                    start=(first and s == 0),
                    stop=(not first and s == 1),
                )

        def wd4_passes(bank, t0, j0, width, first):
            for s in range(2):
                col0 = P * (t0 + s)
                nc.tensor.matmul_mx(
                    out=bank[:, s, :],
                    lhsT=wd4_dealt[:, 2 * col0 : 2 * (col0 + P)].bitcast(FP4X4),
                    lhsT_scale=wd_scale[:, col0 : col0 + P],
                    rhs=h_codes[1][:, j0 : j0 + width].bitcast(FP8X4),
                    rhs_scale=h_scales[1][:, j0 : j0 + width],
                    start=(first and s == 0),
                    stop=(not first and s == 1),
                )

        def output_bank(j0, width, t0, on_vector_engine=False):
            if t0 == 0:
                sums[j0] = ring3.tile([P, 4, width], F32, name="f32_stage", bufs=4, align_bytes=256)
            y = sums[j0]
            order = (wd4_passes, wd8_passes) if width == UNIT else (wd8_passes, wd4_passes)
            bank = psum.tile([P, 2, width], F32, name="up_bank" if t0 else "gate_bank")
            order[0](bank, t0, j0, width, True)
            order[1](bank, t0, j0, width, False)
            if on_vector_engine:
                spread = bias[:, t0 : t0 + 2].unsqueeze(2).to_broadcast([P, 2, width])
                nc.vector.tensor_tensor(y[:, t0 : t0 + 2, :], bank[:], spread, ADD)
            else:
                for t in (t0, t0 + 1):
                    nc.scalar.activation(
                        out=y[:, t, :], in_=bank[:, t - t0, :], func=IDENTITY, bias=bias[:, t : t + 1], scale=1.0
                    )

        def output_sums(j0, width, vector_banks=()):
            output_bank(j0, width, 0, 0 in vector_banks)
            output_bank(j0, width, 2, 2 in vector_banks)
            nc.sync.dma_start(out=y_rows[:, :, j0 : j0 + width], in_=sums[j0][:])

        y_words = {}

        def round_y(j0, width, copy):
            y_words[j0] = ring2.tile([P, 4 * width], BF16, name="y_words", align_bytes=64)
            copy(out=as_words(y_words[j0][:]), in_=as_planes(sums[j0][:]))

        def quantise_y(j0, width, stored):
            places = slice(j0, j0 + width)
            nc.vector.quantize_mx(
                out=y_codes[:, places].bitcast(FP8X4),
                scales=y_scales[:, places],
                in_=y_words[j0][:],
            )
            if stored:
                done = slice(j0 + width - stored, j0 + width)
                nc.sync.dma_start(out=y_word_rows[:, done], in_=y_codes[:, done])

        for unit in units[:2]:
            hidden_unit(0, *unit)
        gate_unit(0, HALF, UNIT)
        gate_unit(0, LAST, UNIT, False)
        up_passes(0, HALF, UNIT)
        up_passes(0, LAST, UNIT)
        prepare_wg(on_vector, 1, 1)
        round_wg(on_gpsimd, 0, 1, 0)
        round_wg(on_scalar, 0, 1, 1)
        quantise_wg(0, 1, 0)
        quantise_wg(0, 1, 1)
        deal_wu(on_scalar, 1)
        for c0 in (0, P):
            product(0, HALF, c0)
        for t0 in (0, 2):
            gelu_bank(0, LAST, UNIT, t0)
        for c0 in (0, P):
            product(0, LAST, c0)
        hidden_unit(1, 0, 256)
        quantise_h(1, 0, 256)
        deal_wd()
        quantise_h(0, 0, 512)
        hidden_unit(1, 256, 256)
        quantise_h(1, 256, 256)
        gate_unit(1, 512, 256)
        output_sums(0, 256, ())
        up_unit(1, 512, 256)
        quantise_h(1, 512, 256)
        round_y(0, 256, on_vector)
        quantise_y(0, 256, 256)
        quantise_h(0, 512, 512)
        gate_unit(1, 768, 128)
        output_sums(256, 256, ())
        up_unit(1, 768, 128)
        quantise_h(1, 768, 128)
        round_y(256, 256, on_vector)
        quantise_y(256, 256, 256)
        gate_unit(1, 896, 128)
        output_sums(512, 128, ())
        up_unit(1, 896, 128)
        quantise_h(1, 896, 128)
        round_y(512, 128, on_vector)
        quantise_y(512, 128, 0)
        output_sums(640, 128, ())
        output_sums(768, 128, ())
        round_y(640, 128, on_vector)
        quantise_y(640, 128, 256)
        output_sums(896, 128, (2,))
        round_y(768, 128, on_vector)
        quantise_y(768, 128, 0)
        round_y(896, 128, on_vector)
        quantise_y(896, 128, 256)

        for row in range(4):
            queue = nc.sync if row % 2 else nc.scalar
            queue.dma_start(out=out_2[0, row:16:4, :].bitcast(I32), in_=y_scales[row:P:32, :].bitcast(I32))
